import numpy as np
import ml_dtypes


def mxq(x, axis, fmt="e4m3"):
    dtype, down = {"e4m3": (ml_dtypes.float8_e4m3fn, 7), "e5m2": (ml_dtypes.float8_e5m2, 14)}[fmt]
    v = np.moveaxis(np.asarray(x, np.float32).astype(ml_dtypes.bfloat16).astype(np.float64), axis, -1)
    blocks = v.reshape(v.shape[:-1] + (-1, 32))
    amax = np.abs(blocks).max(-1, keepdims=True)
    byte = np.maximum(np.where(amax > 0, np.frexp(amax)[1] - 1 + 127, 0) - down, 1)
    scale = np.exp2(byte - 127.0)
    codes = (blocks / scale).astype(np.float32).astype(dtype).astype(np.float64)
    return np.moveaxis((codes * scale).reshape(v.shape), -1, axis)


WIDE = False


def mx_kscale(k):
    if not WIDE:
        return np.ones(k)
    levels = np.array([10, -10, 5, -5, 0])
    if k % 512:
        return np.exp2(np.random.permutation(np.resize(levels, k // 32))).repeat(32)
    a = np.empty((k // 512, 16))
    for p in range(k // 512):
        a[p, :8] = np.random.permutation(np.resize(levels, 8))
        for g in range(8):
            far = levels[np.abs(levels - a[p, g]) >= 10]
            a[p, g + 8] = far[np.random.randint(len(far))]
    return np.exp2(a.ravel()).repeat(32)


def f64(x):
    return np.asarray(x).astype(np.float64)


def striped8(idx):
    return np.concatenate([x.reshape(-1, 16).T for x in idx]).astype(np.uint16)


def runs(offs, k):
    lists = np.stack([offs[16 * r : 16 * r + 16].T.reshape(-1) for r in range(8)]).astype(np.int64)
    return lists[np.arange(k) % 512 // 64]


def pack_weight(w):
    k, n = w.shape
    w = f64(np.asarray(w, np.float32).astype(ml_dtypes.bfloat16)).reshape(k // 32, 32, n)
    amax = np.abs(w).max(1)
    byte = np.clip(np.where(amax > 0, np.frexp(amax)[1] - 1 + 127 - 7, 1), 1, 254)
    scaled = (w * np.exp2(127.0 - byte)[:, None, :]).reshape(k, n).astype(np.float32)
    words = np.ascontiguousarray(scaled.reshape(k // 512, 128, 4, n).transpose(0, 1, 3, 2)).astype(ml_dtypes.float8_e4m3fn).view(np.uint8)
    return words, np.ascontiguousarray(byte.astype(np.uint8).reshape(k // 512, 16, n))


def unpack_weight(words, scales):
    g, p, n, _ = words.shape
    vals = np.ascontiguousarray(words).view(ml_dtypes.float8_e4m3fn).astype(np.float64) * np.repeat(np.exp2(scales.astype(np.float64) - 127.0), 8, axis=1)[..., None]
    return vals.transpose(0, 1, 3, 2).reshape(g * 512, n)


def gelu(v):
    return 0.5 * v * (1.0 + np.tanh(np.sqrt(2.0 / np.pi) * (v + 0.044715 * v**3)))


K, T, S, H, N = 1024, 2048, 1024, 512, 128


def setup_inputs():
    n = np.random.standard_normal
    s = mx_kscale(K)[:, None]
    u = mx_kscale(H)
    packed_xT = pack_weight(n((K, T)) * s)
    return {
        "x_words": packed_xT[0],
        "x_scales": packed_xT[1],
        "w1": (n((K, H)) / np.sqrt(K) / s * u).astype(np.float32),
        "w2": (n((H, N)) / np.sqrt(H) / u[:, None]).astype(np.float32),
        "pos": (0.5 * n((H, S)) * u[:, None]).astype(np.float32),
        "offs": striped8(np.random.randint(0, T, (8, S))),
    }


def reference(x_words, x_scales, w1, w2, pos, offs):
    xq = unpack_weight(x_words, x_scales)[np.arange(K)[:, None], runs(offs, K)]
    h = gelu((mxq(f64(w1), 0, "e4m3").T @ xq) + f64(pos))
    return mxq(f64(w2), 0, "e4m3").T @ mxq(h, 0, "e4m3")

@@ -1,0 +1,181 @@
+from contextlib import ExitStack
+
+import concourse.mybir as mybir
+
+K, T, S, H, N = 1024, 2048, 1024, 512, 128
+FLOPS = 2 * K * H * S + 2 * H * N * S
+
+F32 = mybir.dt.float32
+BF16 = mybir.dt.bfloat16
+I32 = mybir.dt.int32
+U32 = mybir.dt.uint32
+U16 = mybir.dt.uint16
+U8 = mybir.dt.uint8
+FP8X4 = mybir.dt.float8_e4m3fn_x4
+GELU = mybir.ActivationFunctionType.Gelu_apprx_tanh
+ADD = mybir.AluOpType.add
+
+P = 128
+PACK = 4
+PASSES = K // (P * PACK)
+HALF = 512
+PLANE_ROW = 8
+CHUNKS = (256, 256, 256, 128, 128)
+W1_SCALAR_COLS = 40
+
+
+def tile_picked_phpq_gelu_p_kernel(tc, x_words, x_scales, w1, w2, pos, offs, out):
+    nc = tc.nc
+    with ExitStack() as ctx:
+        keep = ctx.enter_context(tc.tile_pool(name="keep", bufs=1))
+        psum = ctx.enter_context(tc.psum_pool(name="psum", bufs=1))
+
+        offsets = keep.tile([P, S // 16], U16, name="offsets")
+        nc.sync.dma_start(offsets[:], offs)
+
+        scale_table = keep.tile([P, T], U8, name="scale_table", align_bytes=64)
+        nc.vector.memset(scale_table[:].bitcast(I32), 0)
+        for e in range(2):
+            nc.scalar.dma_start(
+                scale_table[e:P:PLANE_ROW, :].bitcast(I32),
+                x_scales[:, e:16:2, :].rearrange("z r c -> r z c").bitcast(I32),
+            )
+
+        w1_raw = [keep.tile([P, PACK, H], F32, name="w1_raw%d" % z) for z in range(PASSES)]
+        word_table = [keep.tile([P, T], I32, name="word_table%d" % z) for z in range(PASSES)]
+
+        def load_w1(z):
+            nc.sync.dma_start(w1_raw[z][:], w1[z * 512 : (z + 1) * 512, :].rearrange("(p j) c -> p j c", j=PACK))
+
+        def load_words(z):
+            nc.sync.dma_start(word_table[z][:], x_words[z].rearrange("p c r -> p (c r)").bitcast(I32))
+
+        load_w1(0)
+        load_words(0)
+        load_words(1)
+        load_w1(1)
+
+        picked_scales = keep.tile([P, S], U8, name="picked_scales", tag="late", align_bytes=64)
+        nc.vector.tensor_copy(picked_scales[:], scale_table[:].indirect(offsets[:]))
+        x_planes = keep.tile([P, S], U8, name="x_planes", align_bytes=64)
+        nc.vector.tensor_copy(x_planes[:].bitcast(I32), picked_scales[:].bitcast(I32))
+        for z in range(PASSES):
+            for e in range(2):
+                row = PLANE_ROW * z + e
+                nc.scalar.dma_start(
+                    x_planes[row + 2 : P : 32, :].bitcast(I32),
+                    picked_scales[row + 16 : P : 32, :].bitcast(I32),
+                )
+
+        late = keep.tile([P, PACK * S + PACK * N], F32, name="late", tag="late", align_bytes=64)
+        starts = [sum(CHUNKS[:c]) for c in range(len(CHUNKS))]
+        pos_rows = pos.rearrange("(p t) s -> p t s", t=PACK)
+        pos_sb = [
+            late[:, PACK * s0 : PACK * (s0 + n)].rearrange("p (t n) -> p t n", t=PACK) for s0, n in zip(starts, CHUNKS)
+        ]
+        w2_raw = late[:, PACK * S :].rearrange("p (j n) -> p j n", j=PACK)
+        for c, (s0, n) in enumerate(zip(starts, CHUNKS)):
+            nc.sync.dma_start(pos_sb[c], pos_rows[:, :, s0 : s0 + n])
+            if c == 0:
+                nc.sync.dma_start(w2_raw, w2.rearrange("(p j) n -> p j n", j=PACK))
+
+        w1_bf = [keep.tile([P, PACK, P, PACK], BF16, name="w1_bf%d" % z, align_bytes=64) for z in range(PASSES)]
+        w1_codes = [keep.tile([P, H], U32, name="w1_codes%d" % z, align_bytes=64) for z in range(PASSES)]
+        w1_planes = [keep.tile([P, H], U8, name="w1_planes%d" % z, align_bytes=64) for z in range(PASSES)]
+
+        def cast_w1(z):
+            src = w1_raw[z][:].rearrange("p j (m t) -> p m t j", t=PACK)
+            dst = w1_bf[z][:].rearrange("p t m j -> p m t j")
+            nc.scalar.copy(dst[:, :W1_SCALAR_COLS], src[:, :W1_SCALAR_COLS])
+            nc.vector.tensor_copy(dst[:, W1_SCALAR_COLS:], src[:, W1_SCALAR_COLS:])
+
+        def quantize_w1(z, t0, t1):
+            nc.vector.quantize_mx(
+                out=w1_codes[z][:, t0 * P : t1 * P].bitcast(FP8X4),
+                scales=w1_planes[z][:, t0 * P : t1 * P],
+                in_=w1_bf[z][:, t0:t1].rearrange("p t m j -> p (t m j)"),
+            )
+
+        picked = [
+            [keep.tile([P, HALF], U32, name="picked%d_%d" % (z, g), align_bytes=64) for g in range(2)]
+            for z in range(PASSES)
+        ]
+
+        def gather_words(z, g):
+            cols = HALF // 16
+            nc.vector.tensor_copy(
+                picked[z][g][:], word_table[z][:].bitcast(U32).indirect(offsets[:, g * cols : (g + 1) * cols])
+            )
+
+        acc = [[psum.tile([P, HALF], F32, name="acc%d_%d" % (g, t), tag="bank%d" % (PACK * g + t)) for t in range(PACK)] for g in range(2)]
+
+        def first_product(z, g):
+            for t in range(PACK):
+                nc.tensor.matmul_mx(
+                    out=acc[g][t][:],
+                    lhsT=w1_codes[z][:, t * P : (t + 1) * P].bitcast(FP8X4),
+                    lhsT_scale=w1_planes[z][:, t * P : (t + 1) * P],
+                    rhs=picked[z][g][:].bitcast(FP8X4),
+                    rhs_scale=x_planes[PLANE_ROW * z :, g * HALF : (g + 1) * HALF],
+                    start=(z == 0),
+                    stop=(z == PASSES - 1),
+                )
+
+        cast_w1(0)
+        quantize_w1(0, 0, PACK)
+        for g in range(2):
+            gather_words(0, g)
+            first_product(0, g)
+        for g in range(2):
+            gather_words(1, g)
+        cast_w1(1)
+        quantize_w1(1, 0, 1)
+        quantize_w1(1, 1, 2)
+        quantize_w1(1, 2, 4)
+        for g in range(2):
+            first_product(1, g)
+
+        w2_bf = keep.tile([P, N, PACK], BF16, name="w2_bf", align_bytes=64)
+        w2_codes = keep.tile([P, N], U32, name="w2_codes", align_bytes=64)
+        w2_plane = keep.tile([P, N], U8, name="w2_plane", align_bytes=64)
+        nc.scalar.copy(w2_bf[:], w2_raw.rearrange("p j n -> p n j"))
+
+        sums = [keep.tile([P, PACK, n], F32, name="sums%d" % c) for c, n in enumerate(CHUNKS)]
+        h_bf = [keep.tile([P, n, PACK], BF16, name="h_bf%d" % c, align_bytes=64) for c, n in enumerate(CHUNKS)]
+
+        def hidden(c):
+            g, c0 = divmod(starts[c], HALF)
+            n = CHUNKS[c]
+            for t in range(PACK):
+                nc.vector.tensor_tensor(sums[c][:, t, :], acc[g][t][:, c0 : c0 + n], pos_sb[c][:, t, :], ADD)
+            nc.scalar.activation(h_bf[c][:], sums[c][:].rearrange("p t n -> p n t"), GELU)
+
+        def second_product(c):
+            n = CHUNKS[c]
+            h_codes = keep.tile([P, n], U32, name="h_codes%d" % c, align_bytes=64)
+            h_plane = keep.tile([P, n], U8, name="h_plane%d" % c, align_bytes=64)
+            nc.vector.quantize_mx(
+                out=h_codes[:].bitcast(FP8X4), scales=h_plane[:], in_=h_bf[c][:].rearrange("p n t -> p (n t)")
+            )
+            res = psum.tile([P, n], F32, name="res%d" % c, tag="bank%d" % (c % PACK))
+            nc.tensor.matmul_mx(
+                out=res[:],
+                lhsT=w2_codes[:].bitcast(FP8X4),
+                lhsT_scale=w2_plane[:],
+                rhs=h_codes[:].bitcast(FP8X4),
+                rhs_scale=h_plane[:],
+                start=True,
+                stop=True,
+            )
+            res_sb = keep.tile([P, n], F32, name="res_sb%d" % c)
+            nc.scalar.copy(res_sb[:], res[:])
+            nc.sync.dma_start(out[:, starts[c] : starts[c] + n], res_sb[:])
+
+        hidden(0)
+        nc.vector.quantize_mx(
+            out=w2_codes[:].bitcast(FP8X4), scales=w2_plane[:], in_=w2_bf[:].rearrange("p n j -> p (n j)")
+        )
+        for c in range(1, len(CHUNKS)):
+            hidden(c)
+            second_product(c - 1)
+        second_product(len(CHUNKS) - 1)

@@ -35,59 +35,54 @@ def tile_picked_phpq_gelu_p_kernel(tc, x_words, x_scales, w1, w2, pos, offs, out
 
         scale_table = keep.tile([P, T], U8, name="scale_table", align_bytes=64)
         nc.vector.memset(scale_table[:].bitcast(I32), 0)
+        warm = keep.tile([P, 1], F32, name="warm", tag="word_table0")
+        warm_out = keep.tile([P, 1], F32, name="warm_out", tag="word_table1")
+        nc.gpsimd.memset(warm[:], 0.0)
+        nc.scalar.activation(warm_out[:], warm[:], GELU)
         for e in range(2):
-            nc.scalar.dma_start(
+            nc.sync.dma_start(
                 scale_table[e:P:PLANE_ROW, :].bitcast(I32),
                 x_scales[:, e:16:2, :].rearrange("z r c -> r z c").bitcast(I32),
             )
 
-        w1_raw = [keep.tile([P, PACK, H], F32, name="w1_raw%d" % z) for z in range(PASSES)]
-        word_table = [keep.tile([P, T], I32, name="word_table%d" % z) for z in range(PASSES)]
+        w1_raw = {}
+        word_table = [keep.tile([P, T], I32, name="word_table%d" % z, tag="word_table%d" % z) for z in range(PASSES)]
 
-        def load_w1(z):
-            nc.sync.dma_start(w1_raw[z][:], w1[z * 512 : (z + 1) * 512, :].rearrange("(p j) c -> p j c", j=PACK))
+        def load_w1(z, parts):
+            w1_raw[z] = keep.tile([P, parts, PACK, H // parts], F32, name="w1_raw%d" % z, tag="w1_raw")
+            rows = w1[z * 512 : (z + 1) * 512, :].rearrange("(p j) (a c) -> p a j c", j=PACK, a=parts)
+            for a in range(parts):
+                nc.sync.dma_start(w1_raw[z][:, a], rows[:, a])
 
         def load_words(z):
             nc.sync.dma_start(word_table[z][:], x_words[z].rearrange("p c r -> p (c r)").bitcast(I32))
 
-        load_w1(0)
+        load_w1(0, 1)
         load_words(0)
         load_words(1)
-        load_w1(1)
 
-        picked_scales = keep.tile([P, S], U8, name="picked_scales", tag="late", align_bytes=64)
+        picked_scales = keep.tile([P, S], U8, name="picked_scales", align_bytes=64)
         nc.vector.tensor_copy(picked_scales[:], scale_table[:].indirect(offsets[:]))
         x_planes = keep.tile([P, S], U8, name="x_planes", align_bytes=64)
         nc.vector.tensor_copy(x_planes[:].bitcast(I32), picked_scales[:].bitcast(I32))
         for z in range(PASSES):
             for e in range(2):
                 row = PLANE_ROW * z + e
-                nc.scalar.dma_start(
+                nc.sync.dma_start(
                     x_planes[row + 2 : P : 32, :].bitcast(I32),
                     picked_scales[row + 16 : P : 32, :].bitcast(I32),
                 )
 
-        late = keep.tile([P, PACK * S + PACK * N], F32, name="late", tag="late", align_bytes=64)
-        starts = [sum(CHUNKS[:c]) for c in range(len(CHUNKS))]
-        pos_rows = pos.rearrange("(p t) s -> p t s", t=PACK)
-        pos_sb = [
-            late[:, PACK * s0 : PACK * (s0 + n)].rearrange("p (t n) -> p t n", t=PACK) for s0, n in zip(starts, CHUNKS)
-        ]
-        w2_raw = late[:, PACK * S :].rearrange("p (j n) -> p j n", j=PACK)
-        for c, (s0, n) in enumerate(zip(starts, CHUNKS)):
-            nc.sync.dma_start(pos_sb[c], pos_rows[:, :, s0 : s0 + n])
-            if c == 0:
-                nc.sync.dma_start(w2_raw, w2.rearrange("(p j) n -> p j n", j=PACK))
-
-        w1_bf = [keep.tile([P, PACK, P, PACK], BF16, name="w1_bf%d" % z, align_bytes=64) for z in range(PASSES)]
+        w1_bf = [keep.tile([P, PACK, P, PACK], BF16, name="w1_bf%d" % z, tag="late%d" % z, align_bytes=64) for z in range(PASSES)]
         w1_codes = [keep.tile([P, H], U32, name="w1_codes%d" % z, align_bytes=64) for z in range(PASSES)]
         w1_planes = [keep.tile([P, H], U8, name="w1_planes%d" % z, align_bytes=64) for z in range(PASSES)]
 
-        def cast_w1(z):
-            src = w1_raw[z][:].rearrange("p j (m t) -> p m t j", t=PACK)
-            dst = w1_bf[z][:].rearrange("p t m j -> p m t j")
-            nc.scalar.copy(dst[:, :W1_SCALAR_COLS], src[:, :W1_SCALAR_COLS])
-            nc.vector.tensor_copy(dst[:, W1_SCALAR_COLS:], src[:, W1_SCALAR_COLS:])
+        def cast_w1(z, a, m0, cols, width):
+            src = w1_raw[z][:, a].rearrange("p j (m t) -> p m t j", t=PACK)
+            dst = w1_bf[z][:].rearrange("p t m j -> p m t j")[:, m0 : m0 + width]
+            nc.scalar.copy(dst[:, :cols], src[:, :cols])
+            if cols < width:
+                nc.vector.tensor_copy(dst[:, cols:], src[:, cols:])
 
         def quantize_w1(z, t0, t1):
             nc.vector.quantize_mx(
@@ -121,14 +116,29 @@ def tile_picked_phpq_gelu_p_kernel(tc, x_words, x_scales, w1, w2, pos, offs, out
                     stop=(z == PASSES - 1),
                 )
 
-        cast_w1(0)
+        cast_w1(0, 0, 0, P, P)
+        load_w1(1, 2)
         quantize_w1(0, 0, PACK)
+
+        late = keep.tile([P, PACK * S + PACK * N], F32, name="late", tag="late0", align_bytes=64)
+        starts = [sum(CHUNKS[:c]) for c in range(len(CHUNKS))]
+        pos_rows = pos.rearrange("(p t) s -> p t s", t=PACK)
+        pos_sb = [
+            late[:, PACK * s0 : PACK * (s0 + n)].rearrange("p (t n) -> p t n", t=PACK) for s0, n in zip(starts, CHUNKS)
+        ]
+        w2_raw = late[:, PACK * S :].rearrange("p (j n) -> p j n", j=PACK)
+        for c, (s0, n) in enumerate(zip(starts, CHUNKS)):
+            nc.sync.dma_start(pos_sb[c], pos_rows[:, :, s0 : s0 + n])
+            if c == 0:
+                nc.sync.dma_start(w2_raw, w2.rearrange("(p j) n -> p j n", j=PACK))
+
         for g in range(2):
             gather_words(0, g)
             first_product(0, g)
         for g in range(2):
             gather_words(1, g)
-        cast_w1(1)
+        cast_w1(1, 0, 0, 64, 64)
+        cast_w1(1, 1, 64, W1_SCALAR_COLS, 64)
         quantize_w1(1, 0, 1)
         quantize_w1(1, 1, 2)
         quantize_w1(1, 2, 4)
@@ -146,9 +156,15 @@ def tile_picked_phpq_gelu_p_kernel(tc, x_words, x_scales, w1, w2, pos, offs, out
         def hidden(c):
             g, c0 = divmod(starts[c], HALF)
             n = CHUNKS[c]
-            for t in range(PACK):
-                nc.vector.tensor_tensor(sums[c][:, t, :], acc[g][t][:, c0 : c0 + n], pos_sb[c][:, t, :], ADD)
-            nc.scalar.activation(h_bf[c][:], sums[c][:].rearrange("p t n -> p n t"), GELU)
+            step = 128 if c == 0 else n
+            for a in range(0, n, step):
+                for t in range(PACK):
+                    nc.vector.tensor_tensor(
+                        sums[c][:, t, a : a + step], acc[g][t][:, c0 + a : c0 + a + step], pos_sb[c][:, t, a : a + step], ADD
+                    )
+                nc.scalar.activation(
+                    h_bf[c][:, a : a + step], sums[c][:, :, a : a + step].rearrange("p t n -> p n t"), GELU
+                )
 
         def second_product(c):
             n = CHUNKS[c]

@@ -21,7 +21,7 @@ PASSES = K // (P * PACK)
 HALF = 512
 PLANE_ROW = 8
 CHUNKS = (256, 256, 256, 128, 128)
-W1_SCALAR_COLS = 40
+W1_SCALAR_COLS = 32
 
 
 def tile_picked_phpq_gelu_p_kernel(tc, x_words, x_scales, w1, w2, pos, offs, out):
@@ -68,7 +68,7 @@ def tile_picked_phpq_gelu_p_kernel(tc, x_words, x_scales, w1, w2, pos, offs, out
         for z in range(PASSES):
             for e in range(2):
                 row = PLANE_ROW * z + e
-                nc.sync.dma_start(
+                (nc.sync if z == 0 else nc.scalar).dma_start(
                     x_planes[row + 2 : P : 32, :].bitcast(I32),
                     picked_scales[row + 16 : P : 32, :].bitcast(I32),
                 )
@@ -163,7 +163,9 @@ def tile_picked_phpq_gelu_p_kernel(tc, x_words, x_scales, w1, w2, pos, offs, out
                         sums[c][:, t, a : a + step], acc[g][t][:, c0 + a : c0 + a + step], pos_sb[c][:, t, a : a + step], ADD
                     )
                 nc.scalar.activation(
-                    h_bf[c][:, a : a + step], sums[c][:, :, a : a + step].rearrange("p t n -> p n t"), GELU
+                    h_bf[c][:, a : a + step].rearrange("p (q i) t -> p q t i", i=4),
+                    sums[c][:, :, a : a + step].rearrange("p t (q i) -> p q t i", i=4),
+                    GELU,
                 )
 
         def second_product(c):
@@ -184,7 +186,7 @@ def tile_picked_phpq_gelu_p_kernel(tc, x_words, x_scales, w1, w2, pos, offs, out
                 stop=True,
             )
             res_sb = keep.tile([P, n], F32, name="res_sb%d" % c)
-            nc.scalar.copy(res_sb[:], res[:])
+            (nc.scalar.copy if c < 2 else nc.vector.tensor_copy)(res_sb[:], res[:])
             nc.sync.dma_start(out[:, starts[c] : starts[c] + n], res_sb[:])
 
         hidden(0)

@@ -20,25 +20,39 @@ PACK = 4
 PASSES = K // (P * PACK)
 HALF = 512
 PLANE_ROW = 8
+POS_LOADS = (128, 128, 256, 256, 256)
+STEPS = (128, 128, 256, 256, 128, 128)
 CHUNKS = (256, 256, 256, 128, 128)
+SCALAR_STORES = (0, 1)
 W1_SCALAR_COLS = 32
+
+
+def spans(widths):
+    return [(sum(widths[:c]), n) for c, n in enumerate(widths)]
+
+
+def locate(widths, s0):
+    c = max(c for c, (start, n) in enumerate(spans(widths)) if start <= s0)
+    return c, s0 - spans(widths)[c][0]
 
 
 def tile_picked_phpq_gelu_p_kernel(tc, x_words, x_scales, w1, w2, pos, offs, out):
     nc = tc.nc
     with ExitStack() as ctx:
         keep = ctx.enter_context(tc.tile_pool(name="keep", bufs=1))
+        shared = ctx.enter_context(tc.tile_pool(name="shared", bufs=1))
         psum = ctx.enter_context(tc.psum_pool(name="psum", bufs=1))
 
         offsets = keep.tile([P, S // 16], U16, name="offsets")
         nc.sync.dma_start(offsets[:], offs)
 
-        scale_table = keep.tile([P, T], U8, name="scale_table", align_bytes=64)
+        scale_table = keep.tile([P, T], U8, name="scale_table", tag="scale_table", align_bytes=64)
         nc.vector.memset(scale_table[:].bitcast(I32), 0)
-        warm = keep.tile([P, 1], F32, name="warm", tag="word_table0")
-        warm_out = keep.tile([P, 1], F32, name="warm_out", tag="word_table1")
-        nc.gpsimd.memset(warm[:], 0.0)
-        nc.scalar.activation(warm_out[:], warm[:], GELU)
+        half_w1 = PACK * H // 2
+        first = keep.tile([P, 2 * half_w1 + 8], F32, name="first")
+        warm_out = keep.tile([P, 1], F32, name="warm_out", tag="word_table0", align_bytes=64)
+        nc.vector.memset(first[:, half_w1 - 8 : half_w1 + 16], 0.0)
+        nc.scalar.activation(warm_out[:], first[:, half_w1 : half_w1 + 1], GELU)
         for e in range(2):
             nc.sync.dma_start(
                 scale_table[e:P:PLANE_ROW, :].bitcast(I32),
@@ -46,40 +60,50 @@ def tile_picked_phpq_gelu_p_kernel(tc, x_words, x_scales, w1, w2, pos, offs, out
             )
 
         w1_raw = {}
-        word_table = [keep.tile([P, T], I32, name="word_table%d" % z, tag="word_table%d" % z) for z in range(PASSES)]
+        word_table = {}
 
-        def load_w1(z, parts):
-            w1_raw[z] = keep.tile([P, parts, PACK, H // parts], F32, name="w1_raw%d" % z, tag="w1_raw")
-            rows = w1[z * 512 : (z + 1) * 512, :].rearrange("(p j) (a c) -> p a j c", j=PACK, a=parts)
-            for a in range(parts):
-                nc.sync.dma_start(w1_raw[z][:, a], rows[:, a])
+        def load_w1(z, a, flat):
+            w1_raw[z, a] = flat.rearrange("p (j c) -> p j c", j=PACK)
+            rows = w1[z * 512 : (z + 1) * 512, :].rearrange("(p j) (a c) -> p a j c", j=PACK, a=2)
+            nc.sync.dma_start(w1_raw[z, a], rows[:, a])
 
         def load_words(z):
+            if z == 0:
+                word_table[z] = keep.tile([P, T], I32, name="word_table0", tag="word_table0", align_bytes=64)
+            else:
+                word_table[z] = shared.tile([P, T], I32, name="word_table1", align_bytes=64, offset=0)
             nc.sync.dma_start(word_table[z][:], x_words[z].rearrange("p c r -> p (c r)").bitcast(I32))
 
-        load_w1(0, 1)
+        load_w1(0, 0, first[:, :half_w1])
+        load_w1(0, 1, first[:, half_w1 + 8 :])
         load_words(0)
-        load_words(1)
 
-        picked_scales = keep.tile([P, S], U8, name="picked_scales", align_bytes=64)
-        nc.vector.tensor_copy(picked_scales[:], scale_table[:].indirect(offsets[:]))
-        x_planes = keep.tile([P, S], U8, name="x_planes", align_bytes=64)
-        nc.vector.tensor_copy(x_planes[:].bitcast(I32), picked_scales[:].bitcast(I32))
-        for z in range(PASSES):
-            for e in range(2):
-                row = PLANE_ROW * z + e
-                (nc.sync if z == 0 else nc.scalar).dma_start(
-                    x_planes[row + 2 : P : 32, :].bitcast(I32),
-                    picked_scales[row + 16 : P : 32, :].bitcast(I32),
-                )
+        x_planes = [keep.tile([P, HALF], U8, name="x_planes%d" % g, align_bytes=64) for g in range(2)]
+
+        def gather_scales(g, offset):
+            cols = HALF // 16
+            picked_scales = shared.tile([P, HALF], U8, name="picked_scales%d" % g, align_bytes=64, offset=offset)
+            nc.vector.tensor_copy(picked_scales[:], scale_table[:].indirect(offsets[:, g * cols : (g + 1) * cols]))
+            nc.vector.tensor_copy(x_planes[g][:].bitcast(I32), picked_scales[:].bitcast(I32))
+            for z in range(PASSES):
+                for e in range(2):
+                    row = PLANE_ROW * z + e
+                    nc.sync.dma_start(
+                        x_planes[g][row + 2 : P : 32, :].bitcast(I32),
+                        x_planes[g][row + 16 : P : 32, :].bitcast(I32),
+                    )
+
+        gather_scales(0, 4 * T - HALF // 2)
+        load_words(1)
+        gather_scales(1, 4 * T)
 
         w1_bf = [keep.tile([P, PACK, P, PACK], BF16, name="w1_bf%d" % z, tag="late%d" % z, align_bytes=64) for z in range(PASSES)]
         w1_codes = [keep.tile([P, H], U32, name="w1_codes%d" % z, align_bytes=64) for z in range(PASSES)]
         w1_planes = [keep.tile([P, H], U8, name="w1_planes%d" % z, align_bytes=64) for z in range(PASSES)]
 
         def cast_w1(z, a, m0, cols, width):
-            src = w1_raw[z][:, a].rearrange("p j (m t) -> p m t j", t=PACK)
-            dst = w1_bf[z][:].rearrange("p t m j -> p m t j")[:, m0 : m0 + width]
+            src = w1_raw[z, a].rearrange("p j (m t) -> p m j t", t=PACK)
+            dst = w1_bf[z][:].rearrange("p t m j -> p m j t")[:, m0 : m0 + width]
             nc.scalar.copy(dst[:, :cols], src[:, :cols])
             if cols < width:
                 nc.vector.tensor_copy(dst[:, cols:], src[:, cols:])
@@ -111,26 +135,27 @@ def tile_picked_phpq_gelu_p_kernel(tc, x_words, x_scales, w1, w2, pos, offs, out
                     lhsT=w1_codes[z][:, t * P : (t + 1) * P].bitcast(FP8X4),
                     lhsT_scale=w1_planes[z][:, t * P : (t + 1) * P],
                     rhs=picked[z][g][:].bitcast(FP8X4),
-                    rhs_scale=x_planes[PLANE_ROW * z :, g * HALF : (g + 1) * HALF],
+                    rhs_scale=x_planes[g][PLANE_ROW * z :, :],
                     start=(z == 0),
                     stop=(z == PASSES - 1),
                 )
 
-        cast_w1(0, 0, 0, P, P)
-        load_w1(1, 2)
+        cast_w1(0, 0, 0, 64, 64)
+        cast_w1(0, 1, 64, 64, 64)
+        second = shared.tile([P, 2 * half_w1 + PACK * N], F32, name="second", align_bytes=64, offset=4 * T + HALF - 64)
+        for a in range(2):
+            load_w1(1, a, second[:, a * half_w1 : (a + 1) * half_w1])
+        w2_raw = second[:, 2 * half_w1 :].rearrange("p (j n) -> p j n", j=PACK)
+        nc.sync.dma_start(w2_raw, w2.rearrange("(p j) n -> p j n", j=PACK))
         quantize_w1(0, 0, PACK)
 
-        late = keep.tile([P, PACK * S + PACK * N], F32, name="late", tag="late0", align_bytes=64)
-        starts = [sum(CHUNKS[:c]) for c in range(len(CHUNKS))]
+        late = keep.tile([P, PACK * S], F32, name="late", tag="late0", align_bytes=64)
         pos_rows = pos.rearrange("(p t) s -> p t s", t=PACK)
-        pos_sb = [
-            late[:, PACK * s0 : PACK * (s0 + n)].rearrange("p (t n) -> p t n", t=PACK) for s0, n in zip(starts, CHUNKS)
-        ]
-        w2_raw = late[:, PACK * S :].rearrange("p (j n) -> p j n", j=PACK)
-        for c, (s0, n) in enumerate(zip(starts, CHUNKS)):
-            nc.sync.dma_start(pos_sb[c], pos_rows[:, :, s0 : s0 + n])
-            if c == 0:
-                nc.sync.dma_start(w2_raw, w2.rearrange("(p j) n -> p j n", j=PACK))
+        pos_sb = []
+        for s0, n in spans(POS_LOADS):
+            piece = late[:, PACK * s0 : PACK * (s0 + n)].rearrange("p (t n) -> p t n", t=PACK)
+            nc.sync.dma_start(piece, pos_rows[:, :, s0 : s0 + n])
+            pos_sb.append(piece)
 
         for g in range(2):
             gather_words(0, g)
@@ -148,36 +173,40 @@ def tile_picked_phpq_gelu_p_kernel(tc, x_words, x_scales, w1, w2, pos, offs, out
         w2_bf = keep.tile([P, N, PACK], BF16, name="w2_bf", align_bytes=64)
         w2_codes = keep.tile([P, N], U32, name="w2_codes", align_bytes=64)
         w2_plane = keep.tile([P, N], U8, name="w2_plane", align_bytes=64)
-        nc.scalar.copy(w2_bf[:], w2_raw.rearrange("p j n -> p n j"))
+        nc.scalar.copy(
+            w2_bf[:].rearrange("p (q i) j -> p q j i", i=4), w2_raw.rearrange("p j (q i) -> p q j i", i=4)
+        )
+        nc.vector.quantize_mx(
+            out=w2_codes[:].bitcast(FP8X4), scales=w2_plane[:], in_=w2_bf[:].rearrange("p n j -> p (n j)")
+        )
 
-        sums = [keep.tile([P, PACK, n], F32, name="sums%d" % c) for c, n in enumerate(CHUNKS)]
+        sums = [keep.tile([P, PACK, n], F32, name="sums%d" % c) for c, n in enumerate(STEPS)]
         h_bf = [keep.tile([P, n, PACK], BF16, name="h_bf%d" % c, align_bytes=64) for c, n in enumerate(CHUNKS)]
 
-        def hidden(c):
-            g, c0 = divmod(starts[c], HALF)
-            n = CHUNKS[c]
-            step = 128 if c == 0 else n
-            for a in range(0, n, step):
-                for t in range(PACK):
-                    nc.vector.tensor_tensor(
-                        sums[c][:, t, a : a + step], acc[g][t][:, c0 + a : c0 + a + step], pos_sb[c][:, t, a : a + step], ADD
-                    )
-                nc.scalar.activation(
-                    h_bf[c][:, a : a + step].rearrange("p (q i) t -> p q t i", i=4),
-                    sums[c][:, :, a : a + step].rearrange("p t (q i) -> p q t i", i=4),
-                    GELU,
+        for step, (s0, n) in enumerate(spans(STEPS)):
+            g, a0 = divmod(s0, HALF)
+            load, p0 = locate(POS_LOADS, s0)
+            c, h0 = locate(CHUNKS, s0)
+            for t in range(PACK):
+                nc.vector.tensor_tensor(
+                    sums[step][:, t], acc[g][t][:, a0 : a0 + n], pos_sb[load][:, t, p0 : p0 + n], ADD
                 )
+            nc.scalar.activation(
+                h_bf[c][:, h0 : h0 + n].rearrange("p (q i) t -> p q t i", i=4),
+                sums[step][:].rearrange("p t (q i) -> p q t i", i=4),
+                GELU,
+            )
 
-        def second_product(c):
-            n = CHUNKS[c]
+        res = {}
+        for c, n in enumerate(CHUNKS):
             h_codes = keep.tile([P, n], U32, name="h_codes%d" % c, align_bytes=64)
             h_plane = keep.tile([P, n], U8, name="h_plane%d" % c, align_bytes=64)
             nc.vector.quantize_mx(
                 out=h_codes[:].bitcast(FP8X4), scales=h_plane[:], in_=h_bf[c][:].rearrange("p n t -> p (n t)")
             )
-            res = psum.tile([P, n], F32, name="res%d" % c, tag="bank%d" % (c % PACK))
+            res[c] = psum.tile([P, n], F32, name="res%d" % c, tag="bank%d" % c)
             nc.tensor.matmul_mx(
-                out=res[:],
+                out=res[c][:],
                 lhsT=w2_codes[:].bitcast(FP8X4),
                 lhsT_scale=w2_plane[:],
                 rhs=h_codes[:].bitcast(FP8X4),
@@ -185,15 +214,7 @@ def tile_picked_phpq_gelu_p_kernel(tc, x_words, x_scales, w1, w2, pos, offs, out
                 start=True,
                 stop=True,
             )
+        for c, (s0, n) in enumerate(spans(CHUNKS)):
             res_sb = keep.tile([P, n], F32, name="res_sb%d" % c)
-            (nc.scalar.copy if c < 2 else nc.vector.tensor_copy)(res_sb[:], res[:])
-            nc.sync.dma_start(out[:, starts[c] : starts[c] + n], res_sb[:])
-
-        hidden(0)
-        nc.vector.quantize_mx(
-            out=w2_codes[:].bitcast(FP8X4), scales=w2_plane[:], in_=w2_bf[:].rearrange("p n j -> p (n j)")
-        )
-        for c in range(1, len(CHUNKS)):
-            hidden(c)
-            second_product(c - 1)
-        second_product(len(CHUNKS) - 1)
+            (nc.scalar.copy if c in SCALAR_STORES else nc.vector.tensor_copy)(res_sb[:], res[c][:])
+            nc.sync.dma_start(out[:, s0 : s0 + n], res_sb[:])

@@ -14,17 +14,19 @@ U8 = mybir.dt.uint8
 FP8X4 = mybir.dt.float8_e4m3fn_x4
 GELU = mybir.ActivationFunctionType.Gelu_apprx_tanh
 ADD = mybir.AluOpType.add
+MULT = mybir.AluOpType.mult
 
 P = 128
 PACK = 4
 PASSES = K // (P * PACK)
-HALF = 512
+BANK = 512
+EDGE = 256
 PLANE_ROW = 8
-POS_LOADS = (128, 128, 256, 256, 256)
+POS_LOADS = (256, 256, 256, 256)
+W2_AFTER = 2
 STEPS = (128, 128, 256, 256, 128, 128)
 CHUNKS = (256, 256, 256, 128, 128)
-SCALAR_STORES = (0, 1)
-W1_SCALAR_COLS = 32
+W1_SCALAR_COLS = 40
 
 
 def spans(widths):
@@ -50,9 +52,9 @@ def tile_picked_phpq_gelu_p_kernel(tc, x_words, x_scales, w1, w2, pos, offs, out
         nc.vector.memset(scale_table[:].bitcast(I32), 0)
         half_w1 = PACK * H // 2
         first = keep.tile([P, 2 * half_w1 + 8], F32, name="first")
-        warm_out = keep.tile([P, 1], F32, name="warm_out", tag="word_table0", align_bytes=64)
+        warm_out = shared.tile([P, 32], F32, name="warm_out", align_bytes=64, offset=4 * T - 64)
         nc.vector.memset(first[:, half_w1 - 8 : half_w1 + 16], 0.0)
-        nc.scalar.activation(warm_out[:], first[:, half_w1 : half_w1 + 1], GELU)
+        nc.scalar.activation(warm_out[:, :1], first[:, half_w1 : half_w1 + 1], GELU)
         for e in range(2):
             nc.sync.dma_start(
                 scale_table[e:P:PLANE_ROW, :].bitcast(I32),
@@ -68,34 +70,25 @@ def tile_picked_phpq_gelu_p_kernel(tc, x_words, x_scales, w1, w2, pos, offs, out
             nc.sync.dma_start(w1_raw[z, a], rows[:, a])
 
         def load_words(z):
-            if z == 0:
-                word_table[z] = keep.tile([P, T], I32, name="word_table0", tag="word_table0", align_bytes=64)
-            else:
-                word_table[z] = shared.tile([P, T], I32, name="word_table1", align_bytes=64, offset=0)
+            word_table[z] = shared.tile([P, T], I32, name="word_table%d" % z, align_bytes=64, offset=4 * T * z)
             nc.sync.dma_start(word_table[z][:], x_words[z].rearrange("p c r -> p (c r)").bitcast(I32))
 
         load_w1(0, 0, first[:, :half_w1])
         load_w1(0, 1, first[:, half_w1 + 8 :])
         load_words(0)
 
-        x_planes = [keep.tile([P, HALF], U8, name="x_planes%d" % g, align_bytes=64) for g in range(2)]
-
-        def gather_scales(g, offset):
-            cols = HALF // 16
-            picked_scales = shared.tile([P, HALF], U8, name="picked_scales%d" % g, align_bytes=64, offset=offset)
-            nc.vector.tensor_copy(picked_scales[:], scale_table[:].indirect(offsets[:, g * cols : (g + 1) * cols]))
-            nc.vector.tensor_copy(x_planes[g][:].bitcast(I32), picked_scales[:].bitcast(I32))
-            for z in range(PASSES):
-                for e in range(2):
-                    row = PLANE_ROW * z + e
-                    nc.sync.dma_start(
-                        x_planes[g][row + 2 : P : 32, :].bitcast(I32),
-                        x_planes[g][row + 16 : P : 32, :].bitcast(I32),
-                    )
-
-        gather_scales(0, 4 * T - HALF // 2)
         load_words(1)
-        gather_scales(1, 4 * T)
+
+        picked_scales = keep.tile([P, S], U8, name="picked_scales", tag="second", align_bytes=64)
+        nc.vector.tensor_copy(picked_scales[:], scale_table[:].indirect(offsets[:]))
+        x_planes = keep.tile([P, S], U8, name="x_planes", align_bytes=64)
+        nc.vector.tensor_copy(x_planes[:].bitcast(I32), picked_scales[:].bitcast(I32))
+        for z in range(PASSES):
+            for e in range(2):
+                row = PLANE_ROW * z + e
+                nc.sync.dma_start(
+                    x_planes[row + 2 : P : 32, :].bitcast(I32), x_planes[row + 16 : P : 32, :].bitcast(I32)
+                )
 
         w1_bf = [keep.tile([P, PACK, P, PACK], BF16, name="w1_bf%d" % z, tag="late%d" % z, align_bytes=64) for z in range(PASSES)]
         w1_codes = [keep.tile([P, H], U32, name="w1_codes%d" % z, align_bytes=64) for z in range(PASSES)]
@@ -108,105 +101,95 @@ def tile_picked_phpq_gelu_p_kernel(tc, x_words, x_scales, w1, w2, pos, offs, out
             if cols < width:
                 nc.vector.tensor_copy(dst[:, cols:], src[:, cols:])
 
-        def quantize_w1(z, t0, t1):
+        def quantize_w1(z, c0, n):
             nc.vector.quantize_mx(
-                out=w1_codes[z][:, t0 * P : t1 * P].bitcast(FP8X4),
-                scales=w1_planes[z][:, t0 * P : t1 * P],
-                in_=w1_bf[z][:, t0:t1].rearrange("p t m j -> p (t m j)"),
+                out=w1_codes[z][:, c0 : c0 + n].bitcast(FP8X4),
+                scales=w1_planes[z][:, c0 : c0 + n],
+                in_=w1_bf[z][:].rearrange("p t m j -> p (t m j)")[:, PACK * c0 : PACK * (c0 + n)],
             )
 
-        picked = [
-            [keep.tile([P, HALF], U32, name="picked%d_%d" % (z, g), align_bytes=64) for g in range(2)]
-            for z in range(PASSES)
-        ]
+        picked = [keep.tile([P, S], U32, name="picked%d" % z, align_bytes=64) for z in range(PASSES)]
 
-        def gather_words(z, g):
-            cols = HALF // 16
-            nc.vector.tensor_copy(
-                picked[z][g][:], word_table[z][:].bitcast(U32).indirect(offsets[:, g * cols : (g + 1) * cols])
+        def gather_words(z):
+            nc.vector.tensor_copy(picked[z][:], word_table[z][:].bitcast(U32).indirect(offsets[:]))
+
+        banks = [psum.tile([P, BANK], F32, name="bank%d" % b) for b in range(2 * PACK)]
+
+        def sums_of(t, s0, n):
+            if s0 < EDGE:
+                return banks[t][:, s0 : s0 + n]
+            if s0 < EDGE + BANK:
+                return banks[PACK + t][:, s0 - EDGE : s0 - EDGE + n]
+            return banks[t][:, s0 - BANK : s0 - BANK + n]
+
+        def first_product(z, t, s0, n):
+            nc.tensor.matmul_mx(
+                out=sums_of(t, s0, n),
+                lhsT=w1_codes[z][:, t * P : (t + 1) * P].bitcast(FP8X4),
+                lhsT_scale=w1_planes[z][:, t * P : (t + 1) * P],
+                rhs=picked[z][:, s0 : s0 + n].bitcast(FP8X4),
+                rhs_scale=x_planes[PLANE_ROW * z :, s0 : s0 + n],
+                start=(z == 0),
+                stop=(z == PASSES - 1),
             )
-
-        acc = [[psum.tile([P, HALF], F32, name="acc%d_%d" % (g, t), tag="bank%d" % (PACK * g + t)) for t in range(PACK)] for g in range(2)]
-
-        def first_product(z, g):
-            for t in range(PACK):
-                nc.tensor.matmul_mx(
-                    out=acc[g][t][:],
-                    lhsT=w1_codes[z][:, t * P : (t + 1) * P].bitcast(FP8X4),
-                    lhsT_scale=w1_planes[z][:, t * P : (t + 1) * P],
-                    rhs=picked[z][g][:].bitcast(FP8X4),
-                    rhs_scale=x_planes[g][PLANE_ROW * z :, :],
-                    start=(z == 0),
-                    stop=(z == PASSES - 1),
-                )
 
         cast_w1(0, 0, 0, 64, 64)
         cast_w1(0, 1, 64, 64, 64)
-        second = shared.tile([P, 2 * half_w1 + PACK * N], F32, name="second", align_bytes=64, offset=4 * T + HALF - 64)
+        second = keep.tile([P, 2 * half_w1], F32, name="second", tag="second", align_bytes=64)
         for a in range(2):
             load_w1(1, a, second[:, a * half_w1 : (a + 1) * half_w1])
-        w2_raw = second[:, 2 * half_w1 :].rearrange("p (j n) -> p j n", j=PACK)
-        nc.sync.dma_start(w2_raw, w2.rearrange("(p j) n -> p j n", j=PACK))
-        quantize_w1(0, 0, PACK)
+        quantize_w1(0, 0, H)
 
-        late = keep.tile([P, PACK * S], F32, name="late", tag="late0", align_bytes=64)
+        late = keep.tile([P, PACK * S + PACK * N], F32, name="late", tag="late0", align_bytes=64)
         pos_rows = pos.rearrange("(p t) s -> p t s", t=PACK)
         pos_sb = []
         for s0, n in spans(POS_LOADS):
             piece = late[:, PACK * s0 : PACK * (s0 + n)].rearrange("p (t n) -> p t n", t=PACK)
             nc.sync.dma_start(piece, pos_rows[:, :, s0 : s0 + n])
             pos_sb.append(piece)
+            if len(pos_sb) == W2_AFTER:
+                w2_raw = late[:, PACK * S :].rearrange("p (j n) -> p j n", j=PACK)
+                nc.sync.dma_start(w2_raw, w2.rearrange("(p j) n -> p j n", j=PACK))
 
-        for g in range(2):
-            gather_words(0, g)
-            first_product(0, g)
-        for g in range(2):
-            gather_words(1, g)
-        cast_w1(1, 0, 0, 64, 64)
-        cast_w1(1, 1, 64, W1_SCALAR_COLS, 64)
-        quantize_w1(1, 0, 1)
-        quantize_w1(1, 1, 2)
-        quantize_w1(1, 2, 4)
-        for g in range(2):
-            first_product(1, g)
-
-        w2_bf = keep.tile([P, N, PACK], BF16, name="w2_bf", align_bytes=64)
-        w2_codes = keep.tile([P, N], U32, name="w2_codes", align_bytes=64)
-        w2_plane = keep.tile([P, N], U8, name="w2_plane", align_bytes=64)
-        nc.scalar.copy(
-            w2_bf[:].rearrange("p (q i) j -> p q j i", i=4), w2_raw.rearrange("p j (q i) -> p q j i", i=4)
-        )
-        nc.vector.quantize_mx(
-            out=w2_codes[:].bitcast(FP8X4), scales=w2_plane[:], in_=w2_bf[:].rearrange("p n j -> p (n j)")
-        )
+        for z in range(PASSES):
+            gather_words(z)
+            if z == 1:
+                cast_w1(1, 0, 0, 64, 64)
+                cast_w1(1, 1, 64, W1_SCALAR_COLS, 64)
+                for a in range(2):
+                    for t in range(PACK):
+                        quantize_w1(1, t * P + a * 64, 64)
+            for s0, n in ((0, EDGE), (EDGE, BANK)):
+                for t in range(PACK):
+                    first_product(z, t, s0, n)
 
         sums = [keep.tile([P, PACK, n], F32, name="sums%d" % c) for c, n in enumerate(STEPS)]
         h_bf = [keep.tile([P, n, PACK], BF16, name="h_bf%d" % c, align_bytes=64) for c, n in enumerate(CHUNKS)]
+        w2_bf = keep.tile([P, N, PACK], BF16, name="w2_bf", align_bytes=64)
+        w2_codes = keep.tile([P, N], U32, name="w2_codes", align_bytes=64)
+        w2_plane = keep.tile([P, N], U8, name="w2_plane", align_bytes=64)
 
-        for step, (s0, n) in enumerate(spans(STEPS)):
-            g, a0 = divmod(s0, HALF)
+        def hidden(step):
+            s0, n = spans(STEPS)[step]
             load, p0 = locate(POS_LOADS, s0)
             c, h0 = locate(CHUNKS, s0)
             for t in range(PACK):
-                nc.vector.tensor_tensor(
-                    sums[step][:, t], acc[g][t][:, a0 : a0 + n], pos_sb[load][:, t, p0 : p0 + n], ADD
-                )
+                nc.vector.tensor_tensor(sums[step][:, t], sums_of(t, s0, n), pos_sb[load][:, t, p0 : p0 + n], ADD)
             nc.scalar.activation(
                 h_bf[c][:, h0 : h0 + n].rearrange("p (q i) t -> p q t i", i=4),
                 sums[step][:].rearrange("p t (q i) -> p q t i", i=4),
                 GELU,
             )
 
-        res = {}
-        for c, n in enumerate(CHUNKS):
+        def second_product(c, bank):
+            s0, n = spans(CHUNKS)[c]
             h_codes = keep.tile([P, n], U32, name="h_codes%d" % c, align_bytes=64)
             h_plane = keep.tile([P, n], U8, name="h_plane%d" % c, align_bytes=64)
             nc.vector.quantize_mx(
                 out=h_codes[:].bitcast(FP8X4), scales=h_plane[:], in_=h_bf[c][:].rearrange("p n t -> p (n t)")
             )
-            res[c] = psum.tile([P, n], F32, name="res%d" % c, tag="bank%d" % c)
             nc.tensor.matmul_mx(
-                out=res[c][:],
+                out=banks[bank][:, :n],
                 lhsT=w2_codes[:].bitcast(FP8X4),
                 lhsT_scale=w2_plane[:],
                 rhs=h_codes[:].bitcast(FP8X4),
@@ -214,7 +197,33 @@ def tile_picked_phpq_gelu_p_kernel(tc, x_words, x_scales, w1, w2, pos, offs, out
                 start=True,
                 stop=True,
             )
-        for c, (s0, n) in enumerate(spans(CHUNKS)):
+
+        def store(c, bank, copy):
+            s0, n = spans(CHUNKS)[c]
             res_sb = keep.tile([P, n], F32, name="res_sb%d" % c)
-            (nc.scalar.copy if c in SCALAR_STORES else nc.vector.tensor_copy)(res_sb[:], res[c][:])
+            copy(res_sb[:], banks[bank][:, :n])
             nc.sync.dma_start(out[:, s0 : s0 + n], res_sb[:])
+
+        hidden(0)
+        hidden(1)
+        for t in range(PACK):
+            for z in range(PASSES):
+                first_product(z, t, EDGE + BANK, EDGE)
+        hidden(2)
+        nc.gpsimd.tensor_scalar(w2_bf[:], w2_raw.rearrange("p j n -> p n j"), 1.0, 0.0, MULT, ADD)
+        nc.vector.quantize_mx(
+            out=w2_codes[:].bitcast(FP8X4), scales=w2_plane[:], in_=w2_bf[:].rearrange("p n j -> p (n j)")
+        )
+        second_product(0, 3)
+        store(0, 3, nc.scalar.copy)
+        hidden(3)
+        second_product(1, PACK)
+        hidden(4)
+        hidden(5)
+        for c in range(2, len(CHUNKS)):
+            second_product(c, PACK + c - 1)
+            if c == 3:
+                store(1, PACK, nc.vector.tensor_copy)
+        store(2, PACK + 1, nc.scalar.copy)
+        store(3, PACK + 2, nc.scalar.copy)
+        store(4, PACK + 3, nc.vector.tensor_copy)

@@ -21,12 +21,13 @@ PACK = 4
 PASSES = K // (P * PACK)
 BANK = 512
 EDGE = 256
+LEAD = 320
 PLANE_ROW = 8
 POS_LOADS = (256, 256, 256, 256)
 W2_AFTER = 2
 STEPS = (128, 128, 256, 256, 128, 128)
 CHUNKS = (256, 256, 256, 128, 128)
-W1_SCALAR_COLS = 40
+W1_SCALAR_COLS = 48
 
 
 def spans(widths):
@@ -51,10 +52,10 @@ def tile_picked_phpq_gelu_p_kernel(tc, x_words, x_scales, w1, w2, pos, offs, out
         scale_table = keep.tile([P, T], U8, name="scale_table", tag="scale_table", align_bytes=64)
         nc.vector.memset(scale_table[:].bitcast(I32), 0)
         half_w1 = PACK * H // 2
-        first = keep.tile([P, 2 * half_w1 + 8], F32, name="first")
-        warm_out = shared.tile([P, 32], F32, name="warm_out", align_bytes=64, offset=4 * T - 64)
-        nc.vector.memset(first[:, half_w1 - 8 : half_w1 + 16], 0.0)
-        nc.scalar.activation(warm_out[:, :1], first[:, half_w1 : half_w1 + 1], GELU)
+        first = keep.tile([P, 8 + PACK * LEAD], F32, name="first")
+        warm_out = shared.tile([P, PACK * (H - LEAD) + 32], F32, name="warm_out", align_bytes=64, offset=4 * T - 64)
+        nc.vector.memset(first[:, :16], 0.0)
+        nc.scalar.activation(warm_out[:, :1], first[:, :1], GELU)
         for e in range(2):
             nc.sync.dma_start(
                 scale_table[e:P:PLANE_ROW, :].bitcast(I32),
@@ -64,19 +65,19 @@ def tile_picked_phpq_gelu_p_kernel(tc, x_words, x_scales, w1, w2, pos, offs, out
         w1_raw = {}
         word_table = {}
 
-        def load_w1(z, a, flat):
+        def load_w1(z, a, flat, c0, c1):
             w1_raw[z, a] = flat.rearrange("p (j c) -> p j c", j=PACK)
-            rows = w1[z * 512 : (z + 1) * 512, :].rearrange("(p j) (a c) -> p a j c", j=PACK, a=2)
-            nc.sync.dma_start(w1_raw[z, a], rows[:, a])
+            rows = w1[z * 512 : (z + 1) * 512, :].rearrange("(p j) c -> p j c", j=PACK)
+            nc.sync.dma_start(w1_raw[z, a], rows[:, :, c0:c1])
 
         def load_words(z):
-            word_table[z] = shared.tile([P, T], I32, name="word_table%d" % z, align_bytes=64, offset=4 * T * z)
+            word_table[z] = shared.tile([P, T], I32, name="word_table%d" % z, align_bytes=64, offset=4 * (T + PACK * (H - LEAD)) * z)
             nc.sync.dma_start(word_table[z][:], x_words[z].rearrange("p c r -> p (c r)").bitcast(I32))
 
-        load_w1(0, 0, first[:, :half_w1])
-        load_w1(0, 1, first[:, half_w1 + 8 :])
+        load_w1(0, 0, first[:, 8:], 0, LEAD)
         load_words(0)
-
+        rest = shared.tile([P, PACK * (H - LEAD)], F32, name="rest", align_bytes=64, offset=4 * T)
+        load_w1(0, 1, rest[:], LEAD, H)
         load_words(1)
 
         picked_scales = keep.tile([P, S], U8, name="picked_scales", tag="second", align_bytes=64)
@@ -108,6 +109,11 @@ def tile_picked_phpq_gelu_p_kernel(tc, x_words, x_scales, w1, w2, pos, offs, out
                 in_=w1_bf[z][:].rearrange("p t m j -> p (t m j)")[:, PACK * c0 : PACK * (c0 + n)],
             )
 
+        def quantize_halves(z):
+            for a in range(2):
+                for t in range(PACK):
+                    quantize_w1(z, t * P + a * 64, 64)
+
         picked = [keep.tile([P, S], U32, name="picked%d" % z, align_bytes=64) for z in range(PASSES)]
 
         def gather_words(z):
@@ -133,12 +139,12 @@ def tile_picked_phpq_gelu_p_kernel(tc, x_words, x_scales, w1, w2, pos, offs, out
                 stop=(z == PASSES - 1),
             )
 
-        cast_w1(0, 0, 0, 64, 64)
-        cast_w1(0, 1, 64, 64, 64)
+        cast_w1(0, 0, 0, LEAD // PACK, LEAD // PACK)
+        cast_w1(0, 1, LEAD // PACK, (H - LEAD) // PACK, (H - LEAD) // PACK)
         second = keep.tile([P, 2 * half_w1], F32, name="second", tag="second", align_bytes=64)
         for a in range(2):
-            load_w1(1, a, second[:, a * half_w1 : (a + 1) * half_w1])
-        quantize_w1(0, 0, H)
+            load_w1(1, a, second[:, a * half_w1 : (a + 1) * half_w1], a * H // 2, (a + 1) * H // 2)
+        quantize_halves(0)
 
         late = keep.tile([P, PACK * S + PACK * N], F32, name="late", tag="late0", align_bytes=64)
         pos_rows = pos.rearrange("(p t) s -> p t s", t=PACK)
@@ -156,9 +162,7 @@ def tile_picked_phpq_gelu_p_kernel(tc, x_words, x_scales, w1, w2, pos, offs, out
             if z == 1:
                 cast_w1(1, 0, 0, 64, 64)
                 cast_w1(1, 1, 64, W1_SCALAR_COLS, 64)
-                for a in range(2):
-                    for t in range(PACK):
-                        quantize_w1(1, t * P + a * 64, 64)
+                quantize_halves(1)
             for s0, n in ((0, EDGE), (EDGE, BANK)):
                 for t in range(PACK):
                     first_product(z, t, s0, n)

@@ -27,7 +27,7 @@ POS_LOADS = (256, 256, 256, 256)
 W2_AFTER = 2
 STEPS = (128, 128, 256, 256, 128, 128)
 CHUNKS = (256, 256, 256, 128, 128)
-W1_SCALAR_COLS = 48
+W1_SCALAR_COLS = 40
 
 
 def spans(widths):
@@ -52,7 +52,7 @@ def tile_picked_phpq_gelu_p_kernel(tc, x_words, x_scales, w1, w2, pos, offs, out
         scale_table = keep.tile([P, T], U8, name="scale_table", tag="scale_table", align_bytes=64)
         nc.vector.memset(scale_table[:].bitcast(I32), 0)
         half_w1 = PACK * H // 2
-        first = keep.tile([P, 8 + PACK * LEAD], F32, name="first")
+        first = keep.tile([P, 8 + PACK * LEAD], F32, name="first", tag="first", align_bytes=64)
         warm_out = shared.tile([P, PACK * (H - LEAD) + 32], F32, name="warm_out", align_bytes=64, offset=4 * T - 64)
         nc.vector.memset(first[:, :16], 0.0)
         nc.scalar.activation(warm_out[:, :1], first[:, :1], GELU)
@@ -80,39 +80,41 @@ def tile_picked_phpq_gelu_p_kernel(tc, x_words, x_scales, w1, w2, pos, offs, out
         load_w1(0, 1, rest[:], LEAD, H)
         load_words(1)
 
-        picked_scales = keep.tile([P, S], U8, name="picked_scales", tag="second", align_bytes=64)
+        picked_scales = keep.tile([P, S], U8, name="picked_scales", tag="plane0", align_bytes=64)
         nc.vector.tensor_copy(picked_scales[:], scale_table[:].indirect(offsets[:]))
-        x_planes = keep.tile([P, S], U8, name="x_planes", align_bytes=64)
-        nc.vector.tensor_copy(x_planes[:].bitcast(I32), picked_scales[:].bitcast(I32))
-        for z in range(PASSES):
+        x_planes = {}
+
+        def spread_scales(z, tag, queue):
+            x_planes[z] = keep.tile([P, S], U8, name="x_planes%d" % z, tag=tag, align_bytes=64)
+            nc.vector.tensor_copy(x_planes[z][:].bitcast(I32), picked_scales[:].bitcast(I32))
             for e in range(2):
                 row = PLANE_ROW * z + e
-                nc.sync.dma_start(
-                    x_planes[row + 2 : P : 32, :].bitcast(I32), x_planes[row + 16 : P : 32, :].bitcast(I32)
+                queue.dma_start(
+                    x_planes[z][row + 2 : P : 32, :].bitcast(I32), x_planes[z][row + 16 : P : 32, :].bitcast(I32)
                 )
 
-        w1_bf = [keep.tile([P, PACK, P, PACK], BF16, name="w1_bf%d" % z, tag="late%d" % z, align_bytes=64) for z in range(PASSES)]
+        spread_scales(0, "x_planes0", nc.sync)
+        w1_bf = {
+            (z, a): keep.tile([P, PACK, 64, PACK], BF16, name="w1_bf%d_%d" % (z, a), tag="late%d_%d" % (z, a), align_bytes=64)
+            for z in range(PASSES)
+            for a in range(2)
+        }
         w1_codes = [keep.tile([P, H], U32, name="w1_codes%d" % z, align_bytes=64) for z in range(PASSES)]
-        w1_planes = [keep.tile([P, H], U8, name="w1_planes%d" % z, align_bytes=64) for z in range(PASSES)]
+        w1_planes = {}
 
-        def cast_w1(z, a, m0, cols, width):
-            src = w1_raw[z, a].rearrange("p j (m t) -> p m j t", t=PACK)
-            dst = w1_bf[z][:].rearrange("p t m j -> p m j t")[:, m0 : m0 + width]
-            nc.scalar.copy(dst[:, :cols], src[:, :cols])
-            if cols < width:
-                nc.vector.tensor_copy(dst[:, cols:], src[:, cols:])
+        def cast_w1(copy, z, piece, m0, half, m1, count):
+            src = w1_raw[z, piece].rearrange("p j (m t) -> p m j t", t=PACK)
+            dst = w1_bf[z, half][:].rearrange("p t m j -> p m j t")
+            copy(dst[:, m1 : m1 + count], src[:, m0 : m0 + count])
 
-        def quantize_w1(z, c0, n):
-            nc.vector.quantize_mx(
-                out=w1_codes[z][:, c0 : c0 + n].bitcast(FP8X4),
-                scales=w1_planes[z][:, c0 : c0 + n],
-                in_=w1_bf[z][:].rearrange("p t m j -> p (t m j)")[:, PACK * c0 : PACK * (c0 + n)],
-            )
-
-        def quantize_halves(z):
-            for a in range(2):
-                for t in range(PACK):
-                    quantize_w1(z, t * P + a * 64, 64)
+        def quantize_w1(z, a):
+            for t in range(PACK):
+                cols = slice(t * P + a * 64, t * P + (a + 1) * 64)
+                nc.vector.quantize_mx(
+                    out=w1_codes[z][:, cols].bitcast(FP8X4),
+                    scales=w1_planes[z][:, cols],
+                    in_=w1_bf[z, a][:, t].rearrange("p m j -> p (m j)"),
+                )
 
         picked = [keep.tile([P, S], U32, name="picked%d" % z, align_bytes=64) for z in range(PASSES)]
 
@@ -134,19 +136,25 @@ def tile_picked_phpq_gelu_p_kernel(tc, x_words, x_scales, w1, w2, pos, offs, out
                 lhsT=w1_codes[z][:, t * P : (t + 1) * P].bitcast(FP8X4),
                 lhsT_scale=w1_planes[z][:, t * P : (t + 1) * P],
                 rhs=picked[z][:, s0 : s0 + n].bitcast(FP8X4),
-                rhs_scale=x_planes[PLANE_ROW * z :, s0 : s0 + n],
+                rhs_scale=x_planes[z][PLANE_ROW * z :, s0 : s0 + n],
                 start=(z == 0),
                 stop=(z == PASSES - 1),
             )
 
-        cast_w1(0, 0, 0, LEAD // PACK, LEAD // PACK)
-        cast_w1(0, 1, LEAD // PACK, (H - LEAD) // PACK, (H - LEAD) // PACK)
-        second = keep.tile([P, 2 * half_w1], F32, name="second", tag="second", align_bytes=64)
-        for a in range(2):
-            load_w1(1, a, second[:, a * half_w1 : (a + 1) * half_w1], a * H // 2, (a + 1) * H // 2)
-        quantize_halves(0)
+        extra = LEAD // PACK - 64
+        cast_w1(nc.scalar.copy, 0, 0, 0, 0, 0, 64)
+        cast_w1(nc.scalar.copy, 0, 0, 64, 1, 0, extra)
+        spread_scales(1, "first", nc.scalar)
+        for z in range(PASSES):
+            w1_planes[z] = keep.tile([P, H], U8, name="w1_planes%d" % z, tag="plane%d" % z, align_bytes=64)
+        cast_w1(nc.scalar.copy, 0, 1, 0, 1, extra, 64 - extra)
+        quantize_w1(0, 0)
+        quantize_w1(0, 1)
 
-        late = keep.tile([P, PACK * S + PACK * N], F32, name="late", tag="late0", align_bytes=64)
+        late = keep.tile([P, PACK * S + PACK * N + 2 * half_w1], F32, name="late", tag="late0_0", align_bytes=64)
+        for a in range(2):
+            at = PACK * S + PACK * N + a * half_w1
+            load_w1(1, a, late[:, at : at + half_w1], a * H // 2, (a + 1) * H // 2)
         pos_rows = pos.rearrange("(p t) s -> p t s", t=PACK)
         pos_sb = []
         for s0, n in spans(POS_LOADS):
@@ -154,15 +162,17 @@ def tile_picked_phpq_gelu_p_kernel(tc, x_words, x_scales, w1, w2, pos, offs, out
             nc.sync.dma_start(piece, pos_rows[:, :, s0 : s0 + n])
             pos_sb.append(piece)
             if len(pos_sb) == W2_AFTER:
-                w2_raw = late[:, PACK * S :].rearrange("p (j n) -> p j n", j=PACK)
+                w2_raw = late[:, PACK * S : PACK * S + PACK * N].rearrange("p (j n) -> p j n", j=PACK)
                 nc.sync.dma_start(w2_raw, w2.rearrange("(p j) n -> p j n", j=PACK))
 
         for z in range(PASSES):
             gather_words(z)
             if z == 1:
-                cast_w1(1, 0, 0, 64, 64)
-                cast_w1(1, 1, 64, W1_SCALAR_COLS, 64)
-                quantize_halves(1)
+                cast_w1(nc.scalar.copy, 1, 0, 0, 0, 0, 64)
+                cast_w1(nc.scalar.copy, 1, 1, 0, 1, 0, W1_SCALAR_COLS)
+                cast_w1(nc.vector.tensor_copy, 1, 1, W1_SCALAR_COLS, 1, W1_SCALAR_COLS, 64 - W1_SCALAR_COLS)
+                quantize_w1(1, 0)
+                quantize_w1(1, 1)
             for s0, n in ((0, EDGE), (EDGE, BANK)):
                 for t in range(PACK):
                     first_product(z, t, s0, n)

@@ -21,11 +21,12 @@ PACK = 4
 PASSES = K // (P * PACK)
 BANK = 512
 EDGE = 256
-LEAD = 320
+AHEAD = 128
+LEAD = 384
 PLANE_ROW = 8
 POS_LOADS = (256, 256, 256, 256)
 W2_AFTER = 2
-STEPS = (128, 128, 256, 256, 128, 128)
+STEPS = (128,) * 8
 CHUNKS = (256, 256, 256, 128, 128)
 W1_SCALAR_COLS = 40
 
@@ -52,7 +53,7 @@ def tile_picked_phpq_gelu_p_kernel(tc, x_words, x_scales, w1, w2, pos, offs, out
         scale_table = keep.tile([P, T], U8, name="scale_table", tag="scale_table", align_bytes=64)
         nc.vector.memset(scale_table[:].bitcast(I32), 0)
         half_w1 = PACK * H // 2
-        first = keep.tile([P, 8 + PACK * LEAD], F32, name="first", tag="first", align_bytes=64)
+        first = keep.tile([P, 8 + PACK * (LEAD - AHEAD)], F32, name="first", tag="first", align_bytes=64)
         warm_out = shared.tile([P, PACK * (H - LEAD) + 32], F32, name="warm_out", align_bytes=64, offset=4 * T - 64)
         nc.vector.memset(first[:, :16], 0.0)
         nc.scalar.activation(warm_out[:, :1], first[:, :1], GELU)
@@ -74,7 +75,9 @@ def tile_picked_phpq_gelu_p_kernel(tc, x_words, x_scales, w1, w2, pos, offs, out
             word_table[z] = shared.tile([P, T], I32, name="word_table%d" % z, align_bytes=64, offset=4 * (T + PACK * (H - LEAD)) * z)
             nc.sync.dma_start(word_table[z][:], x_words[z].rearrange("p c r -> p (c r)").bitcast(I32))
 
-        load_w1(0, 0, first[:, 8:], 0, LEAD)
+        ahead = keep.tile([P, PACK * AHEAD], F32, name="ahead")
+        load_w1(0, 2, ahead[:], 0, AHEAD)
+        load_w1(0, 0, first[:, 8:], AHEAD, LEAD)
         load_words(0)
         rest = shared.tile([P, PACK * (H - LEAD)], F32, name="rest", align_bytes=64, offset=4 * T)
         load_w1(0, 1, rest[:], LEAD, H)
@@ -142,8 +145,9 @@ def tile_picked_phpq_gelu_p_kernel(tc, x_words, x_scales, w1, w2, pos, offs, out
             )
 
         extra = LEAD // PACK - 64
-        cast_w1(nc.scalar.copy, 0, 0, 0, 0, 0, 64)
-        cast_w1(nc.scalar.copy, 0, 0, 64, 1, 0, extra)
+        cast_w1(nc.scalar.copy, 0, 2, 0, 0, 0, AHEAD // PACK)
+        cast_w1(nc.scalar.copy, 0, 0, 0, 0, AHEAD // PACK, 64 - AHEAD // PACK)
+        cast_w1(nc.scalar.copy, 0, 0, 64 - AHEAD // PACK, 1, 0, extra)
         spread_scales(1, "first", nc.scalar)
         for z in range(PASSES):
             w1_planes[z] = keep.tile([P, H], U8, name="w1_planes%d" % z, tag="plane%d" % z, align_bytes=64)
@@ -224,16 +228,18 @@ def tile_picked_phpq_gelu_p_kernel(tc, x_words, x_scales, w1, w2, pos, offs, out
             for z in range(PASSES):
                 first_product(z, t, EDGE + BANK, EDGE)
         hidden(2)
+        hidden(3)
         nc.gpsimd.tensor_scalar(w2_bf[:], w2_raw.rearrange("p j n -> p n j"), 1.0, 0.0, MULT, ADD)
         nc.vector.quantize_mx(
             out=w2_codes[:].bitcast(FP8X4), scales=w2_plane[:], in_=w2_bf[:].rearrange("p n j -> p (n j)")
         )
         second_product(0, 3)
         store(0, 3, nc.scalar.copy)
-        hidden(3)
-        second_product(1, PACK)
         hidden(4)
         hidden(5)
+        second_product(1, PACK)
+        hidden(6)
+        hidden(7)
         for c in range(2, len(CHUNKS)):
             second_product(c, PACK + c - 1)
             if c == 3:

@@ -20,24 +20,20 @@ P = 128
 PACK = 4
 PASSES = K // (P * PACK)
 BANK = 512
-EDGE = 256
-AHEAD = 128
+GROUP = 256
+STEP = 128
+HALF = 64
+AHEAD = 192
 LEAD = 384
 PLANE_ROW = 8
-POS_LOADS = (256, 256, 256, 256)
 W2_AFTER = 2
-STEPS = (128,) * 8
 CHUNKS = (256, 256, 256, 128, 128)
-W1_SCALAR_COLS = 40
+SCALAR_SHARE = (64, 32)
+HELD_BACK = 256
 
 
 def spans(widths):
     return [(sum(widths[:c]), n) for c, n in enumerate(widths)]
-
-
-def locate(widths, s0):
-    c = max(c for c, (start, n) in enumerate(spans(widths)) if start <= s0)
-    return c, s0 - spans(widths)[c][0]
 
 
 def tile_picked_phpq_gelu_p_kernel(tc, x_words, x_scales, w1, w2, pos, offs, out):
@@ -47,203 +43,201 @@ def tile_picked_phpq_gelu_p_kernel(tc, x_words, x_scales, w1, w2, pos, offs, out
         shared = ctx.enter_context(tc.tile_pool(name="shared", bufs=1))
         psum = ctx.enter_context(tc.psum_pool(name="psum", bufs=1))
 
-        offsets = keep.tile([P, S // 16], U16, name="offsets")
-        nc.sync.dma_start(offsets[:], offs)
+        rest_bytes = 4 * PACK * (H - LEAD)
+        table_at = [0, 4 * T + rest_bytes]
+        late_at = table_at[1] + 4 * T
+        piece_bytes = 4 * PACK * GROUP
+        pos_at = late_at + 2 * piece_bytes
+        w2_at = pos_at + 4 * piece_bytes
+        late_bytes = w2_at + 4 * PACK * N - late_at
 
-        scale_table = keep.tile([P, T], U8, name="scale_table", tag="scale_table", align_bytes=64)
+        offsets = keep.tile([P, S // 16], U16, name="offsets")
+        scale_table = keep.tile([P, T], U8, name="scale_table", align_bytes=64)
         nc.vector.memset(scale_table[:].bitcast(I32), 0)
-        half_w1 = PACK * H // 2
-        first = keep.tile([P, 8 + PACK * (LEAD - AHEAD)], F32, name="first", tag="first", align_bytes=64)
-        warm_out = shared.tile([P, PACK * (H - LEAD) + 32], F32, name="warm_out", align_bytes=64, offset=4 * T - 64)
+        first = keep.tile([P, 8 + PACK * (LEAD - AHEAD)], F32, name="first", align_bytes=64)
+        seed = shared.tile([P, rest_bytes // 4 + 32], F32, name="seed", align_bytes=64, offset=4 * T - 64)
+        zero_in = keep.tile([P, 1], F32, name="zero_in")
+        zero_bias = keep.tile([P, 1], F32, name="zero_bias")
         nc.vector.memset(first[:, :16], 0.0)
-        nc.scalar.activation(warm_out[:, :1], first[:, :1], GELU)
+        nc.vector.memset(seed[:, :1], 0.0)
+        nc.vector.tensor_copy(zero_in[:], seed[:, :1])
+        nc.scalar.activation(zero_bias[:], first[:, :1], GELU, bias=zero_in[:])
+
+        def load_w1(z, flat, c0, c1):
+            raw = flat.rearrange("p (j c) -> p j c", j=PACK)
+            rows = w1[z * 512 : (z + 1) * 512, :].rearrange("(p j) c -> p j c", j=PACK)
+            nc.sync.dma_start(raw, rows[:, :, c0:c1])
+            return raw.rearrange("p j (m t) -> p m j t", t=PACK)
+
+        def load_words(z):
+            table = shared.tile([P, T], I32, name="word_table%d" % z, align_bytes=64, offset=table_at[z])
+            nc.sync.dma_start(table[:], x_words[z].rearrange("p c r -> p (c r)").bitcast(I32))
+            return table
+
+        ahead = keep.tile([P, PACK * AHEAD], F32, name="ahead")
+        raw_ahead = load_w1(0, ahead[:], 0, AHEAD)
+        nc.sync.dma_start(offsets[:], offs)
         for e in range(2):
             nc.sync.dma_start(
                 scale_table[e:P:PLANE_ROW, :].bitcast(I32),
                 x_scales[:, e:16:2, :].rearrange("z r c -> r z c").bitcast(I32),
             )
+        raw_first = load_w1(0, first[:, 8:], AHEAD, LEAD)
+        word_table = [load_words(0)]
+        rest = shared.tile([P, rest_bytes // 4], F32, name="rest", align_bytes=64, offset=4 * T)
+        raw_rest = load_w1(0, rest[:], LEAD, H)
+        word_table.append(load_words(1))
 
-        w1_raw = {}
-        word_table = {}
+        picked_scales = shared.tile([P, late_bytes], U8, name="picked_scales", align_bytes=64, offset=late_at)
+        nc.vector.tensor_copy(picked_scales[:, :S], scale_table[:].indirect(offsets[:]))
 
-        def load_w1(z, a, flat, c0, c1):
-            w1_raw[z, a] = flat.rearrange("p (j c) -> p j c", j=PACK)
-            rows = w1[z * 512 : (z + 1) * 512, :].rearrange("(p j) c -> p j c", j=PACK)
-            nc.sync.dma_start(w1_raw[z, a], rows[:, :, c0:c1])
-
-        def load_words(z):
-            word_table[z] = shared.tile([P, T], I32, name="word_table%d" % z, align_bytes=64, offset=4 * (T + PACK * (H - LEAD)) * z)
-            nc.sync.dma_start(word_table[z][:], x_words[z].rearrange("p c r -> p (c r)").bitcast(I32))
-
-        ahead = keep.tile([P, PACK * AHEAD], F32, name="ahead")
-        load_w1(0, 2, ahead[:], 0, AHEAD)
-        load_w1(0, 0, first[:, 8:], AHEAD, LEAD)
-        load_words(0)
-        rest = shared.tile([P, PACK * (H - LEAD)], F32, name="rest", align_bytes=64, offset=4 * T)
-        load_w1(0, 1, rest[:], LEAD, H)
-        load_words(1)
-
-        picked_scales = keep.tile([P, S], U8, name="picked_scales", tag="plane0", align_bytes=64)
-        nc.vector.tensor_copy(picked_scales[:], scale_table[:].indirect(offsets[:]))
-        x_planes = {}
-
-        def spread_scales(z, tag, queue):
-            x_planes[z] = keep.tile([P, S], U8, name="x_planes%d" % z, tag=tag, align_bytes=64)
-            nc.vector.tensor_copy(x_planes[z][:].bitcast(I32), picked_scales[:].bitcast(I32))
-            for e in range(2):
-                row = PLANE_ROW * z + e
-                queue.dma_start(
-                    x_planes[z][row + 2 : P : 32, :].bitcast(I32), x_planes[z][row + 16 : P : 32, :].bitcast(I32)
-                )
-
-        spread_scales(0, "x_planes0", nc.sync)
         w1_bf = {
-            (z, a): keep.tile([P, PACK, 64, PACK], BF16, name="w1_bf%d_%d" % (z, a), tag="late%d_%d" % (z, a), align_bytes=64)
+            (z, a): keep.tile([P, PACK, HALF, PACK], BF16, name="w1_bf%d_%d" % (z, a), tag="half%d_%d" % (z, a), align_bytes=64)
             for z in range(PASSES)
             for a in range(2)
         }
         w1_codes = [keep.tile([P, H], U32, name="w1_codes%d" % z, align_bytes=64) for z in range(PASSES)]
-        w1_planes = {}
+        w1_planes = [keep.tile([P, H], U8, name="w1_planes%d" % z, align_bytes=64) for z in range(PASSES)]
 
-        def cast_w1(copy, z, piece, m0, half, m1, count):
-            src = w1_raw[z, piece].rearrange("p j (m t) -> p m j t", t=PACK)
-            dst = w1_bf[z, half][:].rearrange("p t m j -> p m j t")
-            copy(dst[:, m1 : m1 + count], src[:, m0 : m0 + count])
+        def round_w1(copy, z, raw, first_m, m0, m1):
+            a, at = divmod(m0, HALF)
+            dst = w1_bf[z, a][:].rearrange("p t m j -> p m j t")
+            copy(dst[:, at : at + m1 - m0], raw[:, m0 - first_m : m1 - first_m])
 
         def quantize_w1(z, a):
             for t in range(PACK):
-                cols = slice(t * P + a * 64, t * P + (a + 1) * 64)
+                cols = slice(t * P + a * HALF, t * P + (a + 1) * HALF)
                 nc.vector.quantize_mx(
                     out=w1_codes[z][:, cols].bitcast(FP8X4),
                     scales=w1_planes[z][:, cols],
                     in_=w1_bf[z, a][:, t].rearrange("p m j -> p (m j)"),
                 )
 
-        picked = [keep.tile([P, S], U32, name="picked%d" % z, align_bytes=64) for z in range(PASSES)]
+        picked = {}
 
-        def gather_words(z):
-            nc.vector.tensor_copy(picked[z][:], word_table[z][:].bitcast(U32).indirect(offsets[:]))
+        def gather_words(z, s0, n, tag):
+            tile = keep.tile([P, n], U32, name="picked%d_%d" % (z, s0), tag=tag, align_bytes=64)
+            nc.vector.tensor_copy(tile[:], word_table[z][:].bitcast(U32).indirect(offsets[:, s0 // 16 : (s0 + n) // 16]))
+            for g in range(s0 // GROUP, (s0 + n) // GROUP):
+                picked[z, g] = tile[:, g * GROUP - s0 : (g + 1) * GROUP - s0]
 
         banks = [psum.tile([P, BANK], F32, name="bank%d" % b) for b in range(2 * PACK)]
 
-        def sums_of(t, s0, n):
-            if s0 < EDGE:
-                return banks[t][:, s0 : s0 + n]
-            if s0 < EDGE + BANK:
-                return banks[PACK + t][:, s0 - EDGE : s0 - EDGE + n]
-            return banks[t][:, s0 - BANK : s0 - BANK + n]
+        def sums_of(t, g):
+            return banks[PACK * (g % 2) + t][:, GROUP * (g // 2) : GROUP * (g // 2 + 1)]
 
-        def first_product(z, t, s0, n):
+        def first_product(z, t, g):
             nc.tensor.matmul_mx(
-                out=sums_of(t, s0, n),
+                out=sums_of(t, g),
                 lhsT=w1_codes[z][:, t * P : (t + 1) * P].bitcast(FP8X4),
                 lhsT_scale=w1_planes[z][:, t * P : (t + 1) * P],
-                rhs=picked[z][:, s0 : s0 + n].bitcast(FP8X4),
-                rhs_scale=x_planes[z][PLANE_ROW * z :, s0 : s0 + n],
+                rhs=picked[z, g].bitcast(FP8X4),
+                rhs_scale=x_planes[PLANE_ROW * z :, g * GROUP : (g + 1) * GROUP],
                 start=(z == 0),
                 stop=(z == PASSES - 1),
             )
 
-        extra = LEAD // PACK - 64
-        cast_w1(nc.scalar.copy, 0, 2, 0, 0, 0, AHEAD // PACK)
-        cast_w1(nc.scalar.copy, 0, 0, 0, 0, AHEAD // PACK, 64 - AHEAD // PACK)
-        cast_w1(nc.scalar.copy, 0, 0, 64 - AHEAD // PACK, 1, 0, extra)
-        spread_scales(1, "first", nc.scalar)
-        for z in range(PASSES):
-            w1_planes[z] = keep.tile([P, H], U8, name="w1_planes%d" % z, tag="plane%d" % z, align_bytes=64)
-        cast_w1(nc.scalar.copy, 0, 1, 0, 1, extra, 64 - extra)
+        m_ahead, m_lead = AHEAD // PACK, LEAD // PACK
+        round_w1(nc.scalar.copy, 0, raw_ahead, 0, 0, m_ahead)
+        round_w1(nc.scalar.copy, 0, raw_first, m_ahead, m_ahead, HALF)
+        round_w1(nc.scalar.copy, 0, raw_first, m_ahead, HALF, m_lead)
+        round_w1(nc.scalar.copy, 0, raw_rest, m_lead, m_lead, P)
         quantize_w1(0, 0)
-        quantize_w1(0, 1)
+        x_planes = keep.tile([P, S], U8, name="x_planes", tag="half0_0", align_bytes=64)
+        nc.vector.tensor_copy(x_planes[:].bitcast(I32), picked_scales[:, :S].bitcast(I32))
+        for z in range(PASSES):
+            for e in range(2):
+                row = PLANE_ROW * z + e
+                nc.sync.dma_start(x_planes[row + 2 : P : 32, :].bitcast(I32), x_planes[row + 16 : P : 32, :].bitcast(I32))
 
-        late = keep.tile([P, PACK * S + PACK * N + 2 * half_w1], F32, name="late", tag="late0_0", align_bytes=64)
+        raw_late = []
         for a in range(2):
-            at = PACK * S + PACK * N + a * half_w1
-            load_w1(1, a, late[:, at : at + half_w1], a * H // 2, (a + 1) * H // 2)
+            half = shared.tile([P, PACK * GROUP], F32, name="w1_late%d" % a, align_bytes=64, offset=late_at + a * piece_bytes)
+            raw_late.append(load_w1(1, half[:], a * H // 2, (a + 1) * H // 2))
         pos_rows = pos.rearrange("(p t) s -> p t s", t=PACK)
         pos_sb = []
-        for s0, n in spans(POS_LOADS):
-            piece = late[:, PACK * s0 : PACK * (s0 + n)].rearrange("p (t n) -> p t n", t=PACK)
-            nc.sync.dma_start(piece, pos_rows[:, :, s0 : s0 + n])
+        for g in range(S // GROUP):
+            piece = shared.tile([P, PACK, GROUP], F32, name="pos%d" % g, align_bytes=64, offset=pos_at + g * piece_bytes)
+            nc.sync.dma_start(piece[:], pos_rows[:, :, g * GROUP : (g + 1) * GROUP])
             pos_sb.append(piece)
             if len(pos_sb) == W2_AFTER:
-                w2_raw = late[:, PACK * S : PACK * S + PACK * N].rearrange("p (j n) -> p j n", j=PACK)
-                nc.sync.dma_start(w2_raw, w2.rearrange("(p j) n -> p j n", j=PACK))
+                w2_raw = shared.tile([P, PACK, N], F32, name="w2_raw", align_bytes=64, offset=w2_at)
+                nc.sync.dma_start(w2_raw[:], w2.rearrange("(p j) n -> p j n", j=PACK))
 
-        for z in range(PASSES):
-            gather_words(z)
-            if z == 1:
-                cast_w1(nc.scalar.copy, 1, 0, 0, 0, 0, 64)
-                cast_w1(nc.scalar.copy, 1, 1, 0, 1, 0, W1_SCALAR_COLS)
-                cast_w1(nc.vector.tensor_copy, 1, 1, W1_SCALAR_COLS, 1, W1_SCALAR_COLS, 64 - W1_SCALAR_COLS)
-                quantize_w1(1, 0)
-                quantize_w1(1, 1)
-            for s0, n in ((0, EDGE), (EDGE, BANK)):
-                for t in range(PACK):
-                    first_product(z, t, s0, n)
+        gather_words(0, 0, S, "picked0")
+        quantize_w1(0, 1)
+        for g in range(2):
+            for t in range(PACK):
+                first_product(0, t, g)
+        gather_words(1, 0, S, "picked1")
+        for a in range(2):
+            split = a * HALF + SCALAR_SHARE[a]
+            round_w1(nc.scalar.copy, 1, raw_late[a], a * HALF, a * HALF, split)
+            if split < (a + 1) * HALF:
+                round_w1(nc.vector.tensor_copy, 1, raw_late[a], a * HALF, split, (a + 1) * HALF)
+            quantize_w1(1, a)
 
-        sums = [keep.tile([P, PACK, n], F32, name="sums%d" % c) for c, n in enumerate(STEPS)]
+        for g in range(2):
+            for t in range(PACK):
+                first_product(1, t, g)
+
+        sums = [keep.tile([P, PACK, STEP], F32, name="sums%d" % c, tag="sums%d" % c, align_bytes=64) for c in range(S // STEP)]
         h_bf = [keep.tile([P, n, PACK], BF16, name="h_bf%d" % c, align_bytes=64) for c, n in enumerate(CHUNKS)]
         w2_bf = keep.tile([P, N, PACK], BF16, name="w2_bf", align_bytes=64)
-        w2_codes = keep.tile([P, N], U32, name="w2_codes", align_bytes=64)
         w2_plane = keep.tile([P, N], U8, name="w2_plane", align_bytes=64)
 
         def hidden(step):
-            s0, n = spans(STEPS)[step]
-            load, p0 = locate(POS_LOADS, s0)
-            c, h0 = locate(CHUNKS, s0)
+            g, at = divmod(step * STEP, GROUP)
+            c = max(c for c, (s0, n) in enumerate(spans(CHUNKS)) if s0 <= step * STEP)
+            h0 = step * STEP - spans(CHUNKS)[c][0]
             for t in range(PACK):
-                nc.vector.tensor_tensor(sums[step][:, t], sums_of(t, s0, n), pos_sb[load][:, t, p0 : p0 + n], ADD)
+                nc.vector.tensor_tensor(sums[step][:, t], sums_of(t, g)[:, at : at + STEP], pos_sb[g][:, t, at : at + STEP], ADD)
             nc.scalar.activation(
-                h_bf[c][:, h0 : h0 + n].rearrange("p (q i) t -> p q t i", i=4),
+                h_bf[c][:, h0 : h0 + STEP].rearrange("p (q i) t -> p q t i", i=4),
                 sums[step][:].rearrange("p t (q i) -> p q t i", i=4),
                 GELU,
+                bias=zero_bias[:],
             )
 
-        def second_product(c, bank):
-            s0, n = spans(CHUNKS)[c]
-            h_codes = keep.tile([P, n], U32, name="h_codes%d" % c, align_bytes=64)
+        def late_group(g):
+            for t in range(PACK):
+                for z in range(PASSES):
+                    first_product(z, t, g)
+
+        def second_product(c, h_codes):
+            n = CHUNKS[c]
             h_plane = keep.tile([P, n], U8, name="h_plane%d" % c, align_bytes=64)
-            nc.vector.quantize_mx(
-                out=h_codes[:].bitcast(FP8X4), scales=h_plane[:], in_=h_bf[c][:].rearrange("p n t -> p (n t)")
-            )
+            nc.vector.quantize_mx(out=h_codes.bitcast(FP8X4), scales=h_plane[:], in_=h_bf[c][:].rearrange("p n t -> p (n t)"))
             nc.tensor.matmul_mx(
-                out=banks[bank][:, :n],
-                lhsT=w2_codes[:].bitcast(FP8X4),
+                out=banks[c][:, :n],
+                lhsT=w2_codes.bitcast(FP8X4),
                 lhsT_scale=w2_plane[:],
-                rhs=h_codes[:].bitcast(FP8X4),
+                rhs=h_codes.bitcast(FP8X4),
                 rhs_scale=h_plane[:],
                 start=True,
                 stop=True,
             )
 
-        def store(c, bank, copy):
+        def store(c, copy):
             s0, n = spans(CHUNKS)[c]
             res_sb = keep.tile([P, n], F32, name="res_sb%d" % c)
-            copy(res_sb[:], banks[bank][:, :n])
+            copy(res_sb[:], banks[c][:, :n])
             nc.sync.dma_start(out[:, s0 : s0 + n], res_sb[:])
 
         hidden(0)
         hidden(1)
-        for t in range(PACK):
-            for z in range(PASSES):
-                first_product(z, t, EDGE + BANK, EDGE)
+        late_group(2)
         hidden(2)
         hidden(3)
-        nc.gpsimd.tensor_scalar(w2_bf[:], w2_raw.rearrange("p j n -> p n j"), 1.0, 0.0, MULT, ADD)
-        nc.vector.quantize_mx(
-            out=w2_codes[:].bitcast(FP8X4), scales=w2_plane[:], in_=w2_bf[:].rearrange("p n j -> p (n j)")
-        )
-        second_product(0, 3)
-        store(0, 3, nc.scalar.copy)
-        hidden(4)
-        hidden(5)
-        second_product(1, PACK)
-        hidden(6)
-        hidden(7)
-        for c in range(2, len(CHUNKS)):
-            second_product(c, PACK + c - 1)
-            if c == 3:
-                store(1, PACK, nc.vector.tensor_copy)
-        store(2, PACK + 1, nc.scalar.copy)
-        store(3, PACK + 2, nc.scalar.copy)
-        store(4, PACK + 3, nc.vector.tensor_copy)
+        late_group(3)
+        nc.gpsimd.tensor_scalar(w2_bf[:], w2_raw[:].rearrange("p j n -> p n j"), 1.0, 0.0, MULT, ADD)
+        w2_tile = keep.tile([P, N], U32, name="w2_codes", align_bytes=64)
+        w2_codes = w2_tile[:]
+        nc.vector.quantize_mx(out=w2_codes.bitcast(FP8X4), scales=w2_plane[:], in_=w2_bf[:].rearrange("p n j -> p (n j)"))
+        for step in range(4, 8):
+            hidden(step)
+        for c in range(len(CHUNKS)):
+            codes = keep.tile([P, CHUNKS[c]], U32, name="codes%d" % c, tag="sums%d" % ((c + 4) % 6), align_bytes=64)
+            second_product(c, codes[:])
+        for c in range(len(CHUNKS)):
+            store(c, nc.vector.tensor_copy if c in (2, 4) else nc.scalar.copy)

@@ -24,7 +24,6 @@ GROUP = 256
 STEP = 128
 HALF = 64
 AHEAD = 192
-LEAD = 384
 PLANE_ROW = 8
 W2_AFTER = 2
 CHUNKS = (256, 256, 256, 128, 128)
@@ -43,8 +42,7 @@ def tile_picked_phpq_gelu_p_kernel(tc, x_words, x_scales, w1, w2, pos, offs, out
         shared = ctx.enter_context(tc.tile_pool(name="shared", bufs=1))
         psum = ctx.enter_context(tc.psum_pool(name="psum", bufs=1))
 
-        rest_bytes = 4 * PACK * (H - LEAD)
-        table_at = [0, 4 * T + rest_bytes]
+        table_at = [0, 4 * T]
         late_at = table_at[1] + 4 * T
         piece_bytes = 4 * PACK * GROUP
         pos_at = late_at + 2 * piece_bytes
@@ -54,8 +52,8 @@ def tile_picked_phpq_gelu_p_kernel(tc, x_words, x_scales, w1, w2, pos, offs, out
         offsets = keep.tile([P, S // 16], U16, name="offsets")
         scale_table = keep.tile([P, T], U8, name="scale_table", align_bytes=64)
         nc.vector.memset(scale_table[:].bitcast(I32), 0)
-        first = keep.tile([P, 8 + PACK * (LEAD - AHEAD)], F32, name="first", align_bytes=64)
-        seed = shared.tile([P, rest_bytes // 4 + 32], F32, name="seed", align_bytes=64, offset=4 * T - 64)
+        first = keep.tile([P, 8 + PACK * (H - AHEAD)], F32, name="first", align_bytes=64)
+        seed = shared.tile([P, 32], F32, name="seed", align_bytes=64, offset=4 * T - 64)
         zero_in = keep.tile([P, 1], F32, name="zero_in")
         zero_bias = keep.tile([P, 1], F32, name="zero_bias")
         nc.vector.memset(first[:, :16], 0.0)
@@ -82,11 +80,8 @@ def tile_picked_phpq_gelu_p_kernel(tc, x_words, x_scales, w1, w2, pos, offs, out
                 scale_table[e:P:PLANE_ROW, :].bitcast(I32),
                 x_scales[:, e:16:2, :].rearrange("z r c -> r z c").bitcast(I32),
             )
-        raw_first = load_w1(0, first[:, 8:], AHEAD, LEAD)
-        word_table = [load_words(0)]
-        rest = shared.tile([P, rest_bytes // 4], F32, name="rest", align_bytes=64, offset=4 * T)
-        raw_rest = load_w1(0, rest[:], LEAD, H)
-        word_table.append(load_words(1))
+        raw_first = load_w1(0, first[:, 8:], AHEAD, H)
+        word_table = [load_words(z) for z in range(PASSES)]
 
         picked_scales = shared.tile([P, late_bytes], U8, name="picked_scales", align_bytes=64, offset=late_at)
         nc.vector.tensor_copy(picked_scales[:, :S], scale_table[:].indirect(offsets[:]))
@@ -113,35 +108,40 @@ def tile_picked_phpq_gelu_p_kernel(tc, x_words, x_scales, w1, w2, pos, offs, out
                     in_=w1_bf[z, a][:, t].rearrange("p m j -> p (m j)"),
                 )
 
-        picked = {}
+        picked = [keep.tile([P, S], U32, name="picked%d" % z, align_bytes=64) for z in range(PASSES)]
 
-        def gather_words(z, s0, n, tag):
-            tile = keep.tile([P, n], U32, name="picked%d_%d" % (z, s0), tag=tag, align_bytes=64)
-            nc.vector.tensor_copy(tile[:], word_table[z][:].bitcast(U32).indirect(offsets[:, s0 // 16 : (s0 + n) // 16]))
-            for g in range(s0 // GROUP, (s0 + n) // GROUP):
-                picked[z, g] = tile[:, g * GROUP - s0 : (g + 1) * GROUP - s0]
+        def gather_words(z):
+            nc.vector.tensor_copy(picked[z][:], word_table[z][:].bitcast(U32).indirect(offsets[:]))
 
         banks = [psum.tile([P, BANK], F32, name="bank%d" % b) for b in range(2 * PACK)]
 
-        def sums_of(t, g):
-            return banks[PACK * (g % 2) + t][:, GROUP * (g // 2) : GROUP * (g // 2 + 1)]
+        def sums_of(t, s0, n):
+            if s0 < GROUP:
+                return banks[t][:, s0 : s0 + n]
+            if s0 < GROUP + BANK:
+                return banks[PACK + t][:, s0 - GROUP : s0 - GROUP + n]
+            return banks[t][:, s0 - BANK : s0 - BANK + n]
 
-        def first_product(z, t, g):
+        def first_product(z, t, s0, n):
             nc.tensor.matmul_mx(
-                out=sums_of(t, g),
+                out=sums_of(t, s0, n),
                 lhsT=w1_codes[z][:, t * P : (t + 1) * P].bitcast(FP8X4),
                 lhsT_scale=w1_planes[z][:, t * P : (t + 1) * P],
-                rhs=picked[z, g].bitcast(FP8X4),
-                rhs_scale=x_planes[PLANE_ROW * z :, g * GROUP : (g + 1) * GROUP],
+                rhs=picked[z][:, s0 : s0 + n].bitcast(FP8X4),
+                rhs_scale=x_planes[PLANE_ROW * z :, s0 : s0 + n],
                 start=(z == 0),
                 stop=(z == PASSES - 1),
             )
 
-        m_ahead, m_lead = AHEAD // PACK, LEAD // PACK
+        def early_groups(z):
+            for s0, n in ((0, GROUP), (GROUP, BANK)):
+                for t in range(PACK):
+                    first_product(z, t, s0, n)
+
+        m_ahead = AHEAD // PACK
         round_w1(nc.scalar.copy, 0, raw_ahead, 0, 0, m_ahead)
         round_w1(nc.scalar.copy, 0, raw_first, m_ahead, m_ahead, HALF)
-        round_w1(nc.scalar.copy, 0, raw_first, m_ahead, HALF, m_lead)
-        round_w1(nc.scalar.copy, 0, raw_rest, m_lead, m_lead, P)
+        round_w1(nc.scalar.copy, 0, raw_first, m_ahead, HALF, P)
         quantize_w1(0, 0)
         x_planes = keep.tile([P, S], U8, name="x_planes", tag="half0_0", align_bytes=64)
         nc.vector.tensor_copy(x_planes[:].bitcast(I32), picked_scales[:, :S].bitcast(I32))
@@ -164,22 +164,17 @@ def tile_picked_phpq_gelu_p_kernel(tc, x_words, x_scales, w1, w2, pos, offs, out
                 w2_raw = shared.tile([P, PACK, N], F32, name="w2_raw", align_bytes=64, offset=w2_at)
                 nc.sync.dma_start(w2_raw[:], w2.rearrange("(p j) n -> p j n", j=PACK))
 
-        gather_words(0, 0, S, "picked0")
         quantize_w1(0, 1)
-        for g in range(2):
-            for t in range(PACK):
-                first_product(0, t, g)
-        gather_words(1, 0, S, "picked1")
+        gather_words(0)
+        early_groups(0)
+        gather_words(1)
         for a in range(2):
             split = a * HALF + SCALAR_SHARE[a]
             round_w1(nc.scalar.copy, 1, raw_late[a], a * HALF, a * HALF, split)
             if split < (a + 1) * HALF:
                 round_w1(nc.vector.tensor_copy, 1, raw_late[a], a * HALF, split, (a + 1) * HALF)
             quantize_w1(1, a)
-
-        for g in range(2):
-            for t in range(PACK):
-                first_product(1, t, g)
+        early_groups(1)
 
         sums = [keep.tile([P, PACK, STEP], F32, name="sums%d" % c, tag="sums%d" % c, align_bytes=64) for c in range(S // STEP)]
         h_bf = [keep.tile([P, n, PACK], BF16, name="h_bf%d" % c, align_bytes=64) for c, n in enumerate(CHUNKS)]
@@ -191,7 +186,7 @@ def tile_picked_phpq_gelu_p_kernel(tc, x_words, x_scales, w1, w2, pos, offs, out
             c = max(c for c, (s0, n) in enumerate(spans(CHUNKS)) if s0 <= step * STEP)
             h0 = step * STEP - spans(CHUNKS)[c][0]
             for t in range(PACK):
-                nc.vector.tensor_tensor(sums[step][:, t], sums_of(t, g)[:, at : at + STEP], pos_sb[g][:, t, at : at + STEP], ADD)
+                nc.vector.tensor_tensor(sums[step][:, t], sums_of(t, step * STEP, STEP), pos_sb[g][:, t, at : at + STEP], ADD)
             nc.scalar.activation(
                 h_bf[c][:, h0 : h0 + STEP].rearrange("p (q i) t -> p q t i", i=4),
                 sums[step][:].rearrange("p t (q i) -> p q t i", i=4),
@@ -199,17 +194,17 @@ def tile_picked_phpq_gelu_p_kernel(tc, x_words, x_scales, w1, w2, pos, offs, out
                 bias=zero_bias[:],
             )
 
-        def late_group(g):
+        def late_group():
             for t in range(PACK):
                 for z in range(PASSES):
-                    first_product(z, t, g)
+                    first_product(z, t, GROUP + BANK, GROUP)
 
         def second_product(c, h_codes):
             n = CHUNKS[c]
             h_plane = keep.tile([P, n], U8, name="h_plane%d" % c, align_bytes=64)
             nc.vector.quantize_mx(out=h_codes.bitcast(FP8X4), scales=h_plane[:], in_=h_bf[c][:].rearrange("p n t -> p (n t)"))
             nc.tensor.matmul_mx(
-                out=banks[c][:, :n],
+                out=banks[c + 3][:, :n],
                 lhsT=w2_codes.bitcast(FP8X4),
                 lhsT_scale=w2_plane[:],
                 rhs=h_codes.bitcast(FP8X4),
@@ -221,23 +216,30 @@ def tile_picked_phpq_gelu_p_kernel(tc, x_words, x_scales, w1, w2, pos, offs, out
         def store(c, copy):
             s0, n = spans(CHUNKS)[c]
             res_sb = keep.tile([P, n], F32, name="res_sb%d" % c)
-            copy(res_sb[:], banks[c][:, :n])
+            copy(res_sb[:], banks[c + 3][:, :n])
             nc.sync.dma_start(out[:, s0 : s0 + n], res_sb[:])
 
+        codes = [keep.tile([P, n], U32, name="codes%d" % c, align_bytes=64) for c, n in enumerate(CHUNKS)]
         hidden(0)
         hidden(1)
-        late_group(2)
+        late_group()
         hidden(2)
         hidden(3)
-        late_group(3)
         nc.gpsimd.tensor_scalar(w2_bf[:], w2_raw[:].rearrange("p j n -> p n j"), 1.0, 0.0, MULT, ADD)
         w2_tile = keep.tile([P, N], U32, name="w2_codes", align_bytes=64)
         w2_codes = w2_tile[:]
         nc.vector.quantize_mx(out=w2_codes.bitcast(FP8X4), scales=w2_plane[:], in_=w2_bf[:].rearrange("p n j -> p (n j)"))
-        for step in range(4, 8):
-            hidden(step)
-        for c in range(len(CHUNKS)):
-            codes = keep.tile([P, CHUNKS[c]], U32, name="codes%d" % c, tag="sums%d" % ((c + 4) % 6), align_bytes=64)
-            second_product(c, codes[:])
-        for c in range(len(CHUNKS)):
-            store(c, nc.vector.tensor_copy if c in (2, 4) else nc.scalar.copy)
+        second_product(0, codes[0][:])
+        store(0, nc.scalar.copy)
+        hidden(4)
+        hidden(5)
+        second_product(1, codes[1][:])
+        hidden(6)
+        hidden(7)
+        second_product(2, codes[2][:])
+        second_product(3, codes[3][:])
+        store(1, nc.vector.tensor_copy)
+        second_product(4, codes[4][:])
+        store(2, nc.scalar.copy)
+        store(3, nc.scalar.copy)
+        store(4, nc.vector.tensor_copy)

@@ -20,19 +20,29 @@ P = 128
 PACK = 4
 PASSES = K // (P * PACK)
 BANK = 512
-GROUP = 256
-STEP = 128
-HALF = 64
-AHEAD = 192
+QUADRANT = 32
+LIST_ROWS = 16
 PLANE_ROW = 8
+HALF = P // 2
+LINE = 8
+
+EDGE = 256
+AHEAD = 192
+SCALAR_M = 32
+POS_LOADS = (256, 256, 256, 128, 128)
+STEPS = (64, 64) + (128,) * 7
 W2_AFTER = 2
 CHUNKS = (256, 256, 256, 128, 128)
-SCALAR_SHARE = (64, 32)
-HELD_BACK = 256
+RESULT_BANK = 3
 
 
 def spans(widths):
     return [(sum(widths[:c]), n) for c, n in enumerate(widths)]
+
+
+def locate(widths, s0):
+    c = max(c for c, (start, n) in enumerate(spans(widths)) if start <= s0)
+    return c, s0 - spans(widths)[c][0]
 
 
 def tile_picked_phpq_gelu_p_kernel(tc, x_words, x_scales, w1, w2, pos, offs, out):
@@ -42,33 +52,34 @@ def tile_picked_phpq_gelu_p_kernel(tc, x_words, x_scales, w1, w2, pos, offs, out
         shared = ctx.enter_context(tc.tile_pool(name="shared", bufs=1))
         psum = ctx.enter_context(tc.psum_pool(name="psum", bufs=1))
 
-        table_at = [0, 4 * T]
-        late_at = table_at[1] + 4 * T
-        piece_bytes = 4 * PACK * GROUP
-        pos_at = late_at + 2 * piece_bytes
-        w2_at = pos_at + 4 * piece_bytes
+        table_bytes = 4 * T
+        late_at = PASSES * table_bytes
+        half_bytes = 4 * PACK * H // 2
+        pos_at = late_at + 2 * half_bytes
+        w2_at = pos_at + 4 * PACK * S
         late_bytes = w2_at + 4 * PACK * N - late_at
 
-        offsets = keep.tile([P, S // 16], U16, name="offsets")
+        offsets = keep.tile([P, S // LIST_ROWS], U16, name="offsets")
         scale_table = keep.tile([P, T], U8, name="scale_table", align_bytes=64)
         nc.vector.memset(scale_table[:].bitcast(I32), 0)
-        first = keep.tile([P, 8 + PACK * (H - AHEAD)], F32, name="first", align_bytes=64)
-        seed = shared.tile([P, 32], F32, name="seed", align_bytes=64, offset=4 * T - 64)
+
+        first = keep.tile([P, LINE + PACK * (H - AHEAD)], F32, name="first", align_bytes=64)
+        seed = shared.tile([P, 32], F32, name="seed", align_bytes=64, offset=table_bytes - 64)
         zero_in = keep.tile([P, 1], F32, name="zero_in")
         zero_bias = keep.tile([P, 1], F32, name="zero_bias")
-        nc.vector.memset(first[:, :16], 0.0)
+        nc.vector.memset(first[:, : 2 * LINE], 0.0)
         nc.vector.memset(seed[:, :1], 0.0)
         nc.vector.tensor_copy(zero_in[:], seed[:, :1])
         nc.scalar.activation(zero_bias[:], first[:, :1], GELU, bias=zero_in[:])
 
         def load_w1(z, flat, c0, c1):
             raw = flat.rearrange("p (j c) -> p j c", j=PACK)
-            rows = w1[z * 512 : (z + 1) * 512, :].rearrange("(p j) c -> p j c", j=PACK)
+            rows = w1[z * P * PACK : (z + 1) * P * PACK, :].rearrange("(p j) c -> p j c", j=PACK)
             nc.sync.dma_start(raw, rows[:, :, c0:c1])
             return raw.rearrange("p j (m t) -> p m j t", t=PACK)
 
         def load_words(z):
-            table = shared.tile([P, T], I32, name="word_table%d" % z, align_bytes=64, offset=table_at[z])
+            table = shared.tile([P, T], I32, name="word_table%d" % z, align_bytes=64, offset=z * table_bytes)
             nc.sync.dma_start(table[:], x_words[z].rearrange("p c r -> p (c r)").bitcast(I32))
             return table
 
@@ -80,24 +91,24 @@ def tile_picked_phpq_gelu_p_kernel(tc, x_words, x_scales, w1, w2, pos, offs, out
                 scale_table[e:P:PLANE_ROW, :].bitcast(I32),
                 x_scales[:, e:16:2, :].rearrange("z r c -> r z c").bitcast(I32),
             )
-        raw_first = load_w1(0, first[:, 8:], AHEAD, H)
+        raw_first = load_w1(0, first[:, LINE:], AHEAD, H)
         word_table = [load_words(z) for z in range(PASSES)]
 
         picked_scales = shared.tile([P, late_bytes], U8, name="picked_scales", align_bytes=64, offset=late_at)
         nc.vector.tensor_copy(picked_scales[:, :S], scale_table[:].indirect(offsets[:]))
 
         w1_bf = {
-            (z, a): keep.tile([P, PACK, HALF, PACK], BF16, name="w1_bf%d_%d" % (z, a), tag="half%d_%d" % (z, a), align_bytes=64)
+            (z, a): keep.tile([P, PACK, HALF, PACK], BF16, name="w1_bf%d_%d" % (z, a), align_bytes=64)
             for z in range(PASSES)
             for a in range(2)
         }
         w1_codes = [keep.tile([P, H], U32, name="w1_codes%d" % z, align_bytes=64) for z in range(PASSES)]
         w1_planes = [keep.tile([P, H], U8, name="w1_planes%d" % z, align_bytes=64) for z in range(PASSES)]
 
-        def round_w1(copy, z, raw, first_m, m0, m1):
+        def round_w1(copy, z, raw, raw_m, m0, m1):
             a, at = divmod(m0, HALF)
             dst = w1_bf[z, a][:].rearrange("p t m j -> p m j t")
-            copy(dst[:, at : at + m1 - m0], raw[:, m0 - first_m : m1 - first_m])
+            copy(dst[:, at : at + m1 - m0], raw[:, m0 - raw_m : m1 - raw_m])
 
         def quantize_w1(z, a):
             for t in range(PACK):
@@ -116,10 +127,10 @@ def tile_picked_phpq_gelu_p_kernel(tc, x_words, x_scales, w1, w2, pos, offs, out
         banks = [psum.tile([P, BANK], F32, name="bank%d" % b) for b in range(2 * PACK)]
 
         def sums_of(t, s0, n):
-            if s0 < GROUP:
+            if s0 < EDGE:
                 return banks[t][:, s0 : s0 + n]
-            if s0 < GROUP + BANK:
-                return banks[PACK + t][:, s0 - GROUP : s0 - GROUP + n]
+            if s0 < EDGE + BANK:
+                return banks[PACK + t][:, s0 - EDGE : s0 - EDGE + n]
             return banks[t][:, s0 - BANK : s0 - BANK + n]
 
         def first_product(z, t, s0, n):
@@ -134,7 +145,7 @@ def tile_picked_phpq_gelu_p_kernel(tc, x_words, x_scales, w1, w2, pos, offs, out
             )
 
         def early_groups(z):
-            for s0, n in ((0, GROUP), (GROUP, BANK)):
+            for s0, n in ((0, EDGE), (EDGE, BANK)):
                 for t in range(PACK):
                     first_product(z, t, s0, n)
 
@@ -143,22 +154,26 @@ def tile_picked_phpq_gelu_p_kernel(tc, x_words, x_scales, w1, w2, pos, offs, out
         round_w1(nc.scalar.copy, 0, raw_first, m_ahead, m_ahead, HALF)
         round_w1(nc.scalar.copy, 0, raw_first, m_ahead, HALF, P)
         quantize_w1(0, 0)
-        x_planes = keep.tile([P, S], U8, name="x_planes", tag="half0_0", align_bytes=64)
+
+        x_planes = keep.tile([P, S], U8, name="x_planes", align_bytes=64)
         nc.vector.tensor_copy(x_planes[:].bitcast(I32), picked_scales[:, :S].bitcast(I32))
         for z in range(PASSES):
             for e in range(2):
                 row = PLANE_ROW * z + e
-                nc.sync.dma_start(x_planes[row + 2 : P : 32, :].bitcast(I32), x_planes[row + 16 : P : 32, :].bitcast(I32))
+                nc.sync.dma_start(
+                    x_planes[row + 2 : P : QUADRANT, :].bitcast(I32),
+                    x_planes[row + LIST_ROWS : P : QUADRANT, :].bitcast(I32),
+                )
 
         raw_late = []
         for a in range(2):
-            half = shared.tile([P, PACK * GROUP], F32, name="w1_late%d" % a, align_bytes=64, offset=late_at + a * piece_bytes)
+            half = shared.tile([P, half_bytes // 4], F32, name="w1_late%d" % a, align_bytes=64, offset=late_at + a * half_bytes)
             raw_late.append(load_w1(1, half[:], a * H // 2, (a + 1) * H // 2))
         pos_rows = pos.rearrange("(p t) s -> p t s", t=PACK)
         pos_sb = []
-        for g in range(S // GROUP):
-            piece = shared.tile([P, PACK, GROUP], F32, name="pos%d" % g, align_bytes=64, offset=pos_at + g * piece_bytes)
-            nc.sync.dma_start(piece[:], pos_rows[:, :, g * GROUP : (g + 1) * GROUP])
+        for s0, n in spans(POS_LOADS):
+            piece = shared.tile([P, PACK, n], F32, name="pos%d" % len(pos_sb), align_bytes=64, offset=pos_at + 4 * PACK * s0)
+            nc.sync.dma_start(piece[:], pos_rows[:, :, s0 : s0 + n])
             pos_sb.append(piece)
             if len(pos_sb) == W2_AFTER:
                 w2_raw = shared.tile([P, PACK, N], F32, name="w2_raw", align_bytes=64, offset=w2_at)
@@ -168,46 +183,43 @@ def tile_picked_phpq_gelu_p_kernel(tc, x_words, x_scales, w1, w2, pos, offs, out
         gather_words(0)
         early_groups(0)
         gather_words(1)
-        for a in range(2):
-            split = a * HALF + SCALAR_SHARE[a]
-            round_w1(nc.scalar.copy, 1, raw_late[a], a * HALF, a * HALF, split)
-            if split < (a + 1) * HALF:
-                round_w1(nc.vector.tensor_copy, 1, raw_late[a], a * HALF, split, (a + 1) * HALF)
-            quantize_w1(1, a)
+        round_w1(nc.scalar.copy, 1, raw_late[0], 0, 0, HALF)
+        quantize_w1(1, 0)
+        round_w1(nc.scalar.copy, 1, raw_late[1], HALF, HALF, HALF + SCALAR_M)
+        round_w1(nc.vector.tensor_copy, 1, raw_late[1], HALF, HALF + SCALAR_M, P)
+        quantize_w1(1, 1)
         early_groups(1)
 
-        sums = [keep.tile([P, PACK, STEP], F32, name="sums%d" % c, tag="sums%d" % c, align_bytes=64) for c in range(S // STEP)]
+        sums = [keep.tile([P, PACK, n], F32, name="sums%d" % c) for c, n in enumerate(STEPS)]
         h_bf = [keep.tile([P, n, PACK], BF16, name="h_bf%d" % c, align_bytes=64) for c, n in enumerate(CHUNKS)]
         w2_bf = keep.tile([P, N, PACK], BF16, name="w2_bf", align_bytes=64)
         w2_plane = keep.tile([P, N], U8, name="w2_plane", align_bytes=64)
 
-        def hidden(step):
-            g, at = divmod(step * STEP, GROUP)
-            c = max(c for c, (s0, n) in enumerate(spans(CHUNKS)) if s0 <= step * STEP)
-            h0 = step * STEP - spans(CHUNKS)[c][0]
-            for t in range(PACK):
-                nc.vector.tensor_tensor(sums[step][:, t], sums_of(t, step * STEP, STEP), pos_sb[g][:, t, at : at + STEP], ADD)
-            nc.scalar.activation(
-                h_bf[c][:, h0 : h0 + STEP].rearrange("p (q i) t -> p q t i", i=4),
-                sums[step][:].rearrange("p t (q i) -> p q t i", i=4),
-                GELU,
-                bias=zero_bias[:],
-            )
+        def hidden(v0, v1):
+            for step, (s0, n) in enumerate(spans(STEPS)):
+                if v0 <= s0 < v1:
+                    load, p0 = locate(POS_LOADS, s0)
+                    c, h0 = locate(CHUNKS, s0)
+                    for t in range(PACK):
+                        nc.vector.tensor_tensor(sums[step][:, t], sums_of(t, s0, n), pos_sb[load][:, t, p0 : p0 + n], ADD)
+                    nc.scalar.activation(
+                        h_bf[c][:, h0 : h0 + n].rearrange("p (q i) t -> p q t i", i=4),
+                        sums[step][:].rearrange("p t (q i) -> p q t i", i=4),
+                        GELU,
+                        bias=zero_bias[:],
+                    )
 
-        def late_group():
-            for t in range(PACK):
-                for z in range(PASSES):
-                    first_product(z, t, GROUP + BANK, GROUP)
-
-        def second_product(c, h_codes):
+        def second_product(c):
             n = CHUNKS[c]
             h_plane = keep.tile([P, n], U8, name="h_plane%d" % c, align_bytes=64)
-            nc.vector.quantize_mx(out=h_codes.bitcast(FP8X4), scales=h_plane[:], in_=h_bf[c][:].rearrange("p n t -> p (n t)"))
+            nc.vector.quantize_mx(
+                out=h_codes[c][:].bitcast(FP8X4), scales=h_plane[:], in_=h_bf[c][:].rearrange("p n t -> p (n t)")
+            )
             nc.tensor.matmul_mx(
-                out=banks[c + 3][:, :n],
-                lhsT=w2_codes.bitcast(FP8X4),
+                out=banks[RESULT_BANK + c][:, :n],
+                lhsT=w2_codes[:].bitcast(FP8X4),
                 lhsT_scale=w2_plane[:],
-                rhs=h_codes.bitcast(FP8X4),
+                rhs=h_codes[c][:].bitcast(FP8X4),
                 rhs_scale=h_plane[:],
                 start=True,
                 stop=True,
@@ -216,30 +228,27 @@ def tile_picked_phpq_gelu_p_kernel(tc, x_words, x_scales, w1, w2, pos, offs, out
         def store(c, copy):
             s0, n = spans(CHUNKS)[c]
             res_sb = keep.tile([P, n], F32, name="res_sb%d" % c)
-            copy(res_sb[:], banks[c + 3][:, :n])
+            copy(res_sb[:], banks[RESULT_BANK + c][:, :n])
             nc.sync.dma_start(out[:, s0 : s0 + n], res_sb[:])
 
-        codes = [keep.tile([P, n], U32, name="codes%d" % c, align_bytes=64) for c, n in enumerate(CHUNKS)]
-        hidden(0)
-        hidden(1)
-        late_group()
-        hidden(2)
-        hidden(3)
+        h_codes = [keep.tile([P, n], U32, name="codes%d" % c, align_bytes=64) for c, n in enumerate(CHUNKS)]
+        hidden(0, EDGE)
+        for t in range(PACK):
+            for z in range(PASSES):
+                first_product(z, t, EDGE + BANK, EDGE)
+        hidden(EDGE, 2 * EDGE)
         nc.gpsimd.tensor_scalar(w2_bf[:], w2_raw[:].rearrange("p j n -> p n j"), 1.0, 0.0, MULT, ADD)
-        w2_tile = keep.tile([P, N], U32, name="w2_codes", align_bytes=64)
-        w2_codes = w2_tile[:]
-        nc.vector.quantize_mx(out=w2_codes.bitcast(FP8X4), scales=w2_plane[:], in_=w2_bf[:].rearrange("p n j -> p (n j)"))
-        second_product(0, codes[0][:])
+        w2_codes = keep.tile([P, N], U32, name="w2_codes", align_bytes=64)
+        nc.vector.quantize_mx(out=w2_codes[:].bitcast(FP8X4), scales=w2_plane[:], in_=w2_bf[:].rearrange("p n j -> p (n j)"))
+        second_product(0)
         store(0, nc.scalar.copy)
-        hidden(4)
-        hidden(5)
-        second_product(1, codes[1][:])
-        hidden(6)
-        hidden(7)
-        second_product(2, codes[2][:])
-        second_product(3, codes[3][:])
+        hidden(2 * EDGE, 3 * EDGE)
+        second_product(1)
+        hidden(3 * EDGE, S)
+        second_product(2)
+        second_product(3)
         store(1, nc.vector.tensor_copy)
-        second_product(4, codes[4][:])
+        second_product(4)
         store(2, nc.scalar.copy)
         store(3, nc.scalar.copy)
         store(4, nc.vector.tensor_copy)

@@ -24,10 +24,8 @@ QUADRANT = 32
 LIST_ROWS = 16
 PLANE_ROW = 8
 HALF = P // 2
-LINE = 8
 
 EDGE = 256
-AHEAD = 192
 SCALAR_M = 32
 POS_LOADS = (256, 256, 256, 128, 128)
 STEPS = (64, 64) + (128,) * 7
@@ -59,18 +57,17 @@ def tile_picked_phpq_gelu_p_kernel(tc, x_words, x_scales, w1, w2, pos, offs, out
         w2_at = pos_at + 4 * PACK * S
         late_bytes = w2_at + 4 * PACK * N - late_at
 
-        offsets = keep.tile([P, S // LIST_ROWS], U16, name="offsets")
-        scale_table = keep.tile([P, T], U8, name="scale_table", align_bytes=64)
-        nc.vector.memset(scale_table[:].bitcast(I32), 0)
-
-        first = keep.tile([P, LINE + PACK * (H - AHEAD)], F32, name="first", align_bytes=64)
+        first = keep.tile([P, PACK * H], F32, name="first", align_bytes=64)
         seed = shared.tile([P, 32], F32, name="seed", align_bytes=64, offset=table_bytes - 64)
         zero_in = keep.tile([P, 1], F32, name="zero_in")
         zero_bias = keep.tile([P, 1], F32, name="zero_bias")
-        nc.vector.memset(first[:, : 2 * LINE], 0.0)
-        nc.vector.memset(seed[:, :1], 0.0)
-        nc.vector.tensor_copy(zero_in[:], seed[:, :1])
-        nc.scalar.activation(zero_bias[:], first[:, :1], GELU, bias=zero_in[:])
+        nc.gpsimd.memset(first[:, 2 * H : 2 * H + 1], 0.0)
+        nc.gpsimd.memset(seed[:, :1], 0.0)
+        offsets = keep.tile([P, S // LIST_ROWS], U16, name="offsets")
+        scale_table = keep.tile([P, T], U8, name="scale_table", align_bytes=64)
+        nc.vector.memset(scale_table[:].bitcast(I32), 0)
+        nc.vector.tensor_tensor(zero_in[:], first[:, 2 * H : 2 * H + 1], seed[:, :1], ADD)
+        nc.scalar.activation(zero_bias[:], zero_in[:], GELU, bias=zero_in[:])
 
         def load_w1(z, flat, c0, c1):
             raw = flat.rearrange("p (j c) -> p j c", j=PACK)
@@ -83,16 +80,18 @@ def tile_picked_phpq_gelu_p_kernel(tc, x_words, x_scales, w1, w2, pos, offs, out
             nc.sync.dma_start(table[:], x_words[z].rearrange("p c r -> p (c r)").bitcast(I32))
             return table
 
-        ahead = keep.tile([P, PACK * AHEAD], F32, name="ahead")
-        raw_ahead = load_w1(0, ahead[:], 0, AHEAD)
+        rows_first = w1[: P * PACK, :].rearrange("(p j) c -> p (j c)", j=PACK)
+        nc.sync.dma_start(first[:, :H], rows_first[:, :H])
         nc.sync.dma_start(offsets[:], offs)
         for e in range(2):
             nc.sync.dma_start(
                 scale_table[e:P:PLANE_ROW, :].bitcast(I32),
                 x_scales[:, e:16:2, :].rearrange("z r c -> r z c").bitcast(I32),
             )
-        raw_first = load_w1(0, first[:, LINE:], AHEAD, H)
-        word_table = [load_words(z) for z in range(PASSES)]
+        word_table = [load_words(0)]
+        nc.sync.dma_start(first[:, H:], rows_first[:, H:])
+        raw_first = first[:].rearrange("p (j m t) -> p m j t", j=PACK, t=PACK)
+        word_table.append(load_words(1))
 
         picked_scales = shared.tile([P, late_bytes], U8, name="picked_scales", align_bytes=64, offset=late_at)
         nc.vector.tensor_copy(picked_scales[:, :S], scale_table[:].indirect(offsets[:]))
@@ -149,11 +148,8 @@ def tile_picked_phpq_gelu_p_kernel(tc, x_words, x_scales, w1, w2, pos, offs, out
                 for t in range(PACK):
                     first_product(z, t, s0, n)
 
-        m_ahead = AHEAD // PACK
-        round_w1(nc.scalar.copy, 0, raw_ahead, 0, 0, m_ahead)
-        round_w1(nc.scalar.copy, 0, raw_first, m_ahead, m_ahead, HALF)
-        round_w1(nc.scalar.copy, 0, raw_first, m_ahead, HALF, P)
-        quantize_w1(0, 0)
+        round_w1(nc.scalar.copy, 0, raw_first, 0, 0, HALF)
+        round_w1(nc.scalar.copy, 0, raw_first, 0, HALF, HALF + SCALAR_M)
 
         x_planes = keep.tile([P, S], U8, name="x_planes", align_bytes=64)
         nc.vector.tensor_copy(x_planes[:].bitcast(I32), picked_scales[:, :S].bitcast(I32))
@@ -179,8 +175,10 @@ def tile_picked_phpq_gelu_p_kernel(tc, x_words, x_scales, w1, w2, pos, offs, out
                 w2_raw = shared.tile([P, PACK, N], F32, name="w2_raw", align_bytes=64, offset=w2_at)
                 nc.sync.dma_start(w2_raw[:], w2.rearrange("(p j) n -> p j n", j=PACK))
 
-        quantize_w1(0, 1)
         gather_words(0)
+        round_w1(nc.vector.tensor_copy, 0, raw_first, 0, HALF + SCALAR_M, P)
+        quantize_w1(0, 0)
+        quantize_w1(0, 1)
         early_groups(0)
         gather_words(1)
         round_w1(nc.scalar.copy, 1, raw_late[0], 0, 0, HALF)

@@ -26,6 +26,9 @@ PLANE_ROW = 8
 HALF = P // 2
 
 EDGE = 256
+GROUP = 256
+GROUPS = S // GROUP
+EARLY = 3
 SCALAR_M = 32
 POS_LOADS = (256, 256, 256, 128, 128)
 STEPS = (64, 64) + (128,) * 7
@@ -123,30 +126,21 @@ def tile_picked_phpq_gelu_p_kernel(tc, x_words, x_scales, w1, w2, pos, offs, out
         def gather_words(z):
             nc.vector.tensor_copy(picked[z][:], word_table[z][:].bitcast(U32).indirect(offsets[:]))
 
-        banks = [psum.tile([P, BANK], F32, name="bank%d" % b) for b in range(2 * PACK)]
+        banks = [psum.tile([P, 2, GROUP], F32, name="bank%d" % b) for b in range(2 * GROUPS)]
 
-        def sums_of(t, s0, n):
-            if s0 < EDGE:
-                return banks[t][:, s0 : s0 + n]
-            if s0 < EDGE + BANK:
-                return banks[PACK + t][:, s0 - EDGE : s0 - EDGE + n]
-            return banks[t][:, s0 - BANK : s0 - BANK + n]
-
-        def first_product(z, t, s0, n):
-            nc.tensor.matmul_mx(
-                out=sums_of(t, s0, n),
-                lhsT=w1_codes[z][:, t * P : (t + 1) * P].bitcast(FP8X4),
-                lhsT_scale=w1_planes[z][:, t * P : (t + 1) * P],
-                rhs=picked[z][:, s0 : s0 + n].bitcast(FP8X4),
-                rhs_scale=x_planes[PLANE_ROW * z :, s0 : s0 + n],
-                start=(z == 0),
-                stop=(z == PASSES - 1),
-            )
-
-        def early_groups(z):
-            for s0, n in ((0, EDGE), (EDGE, BANK)):
-                for t in range(PACK):
-                    first_product(z, t, s0, n)
+        def first_product(z, g, opens):
+            s0 = g * GROUP
+            planes = later_planes[:, s0 - GROUP : s0] if z == 1 and g > 0 else x_planes[:, s0 : s0 + GROUP]
+            for t in range(PACK):
+                nc.tensor.matmul_mx(
+                    out=banks[2 * g + t // 2][:, t % 2],
+                    lhsT=w1_codes[z][:, t * P : (t + 1) * P].bitcast(FP8X4),
+                    lhsT_scale=w1_planes[z][:, t * P : (t + 1) * P],
+                    rhs=picked[z][:, s0 : s0 + GROUP].bitcast(FP8X4),
+                    rhs_scale=planes[PLANE_ROW * z :],
+                    start=(opens and t % 2 == 0),
+                    stop=(not opens and t % 2 == 1),
+                )
 
         round_w1(nc.scalar.copy, 0, raw_first, 0, 0, HALF)
         round_w1(nc.scalar.copy, 0, raw_first, 0, HALF, HALF + SCALAR_M)
@@ -179,14 +173,20 @@ def tile_picked_phpq_gelu_p_kernel(tc, x_words, x_scales, w1, w2, pos, offs, out
         round_w1(nc.vector.tensor_copy, 0, raw_first, 0, HALF + SCALAR_M, P)
         quantize_w1(0, 0)
         quantize_w1(0, 1)
-        early_groups(0)
+        for g in range(EARLY):
+            first_product(0, g, True)
         gather_words(1)
         round_w1(nc.scalar.copy, 1, raw_late[0], 0, 0, HALF)
         quantize_w1(1, 0)
         round_w1(nc.scalar.copy, 1, raw_late[1], HALF, HALF, HALF + SCALAR_M)
         round_w1(nc.vector.tensor_copy, 1, raw_late[1], HALF, HALF + SCALAR_M, P)
         quantize_w1(1, 1)
-        early_groups(1)
+        later_planes = shared.tile([P, S - GROUP], U8, name="later_planes", align_bytes=64, offset=late_at + half_bytes)
+        nc.vector.tensor_copy(later_planes[:].bitcast(I32), x_planes[:, GROUP:].bitcast(I32))
+        for g in range(GROUPS):
+            first_product(1, g, g >= EARLY)
+            if g >= EARLY:
+                first_product(0, g, False)
 
         sums = [keep.tile([P, PACK, n], F32, name="sums%d" % c) for c, n in enumerate(STEPS)]
         h_bf = [keep.tile([P, n, PACK], BF16, name="h_bf%d" % c, align_bytes=64) for c, n in enumerate(CHUNKS)]
@@ -198,8 +198,12 @@ def tile_picked_phpq_gelu_p_kernel(tc, x_words, x_scales, w1, w2, pos, offs, out
                 if v0 <= s0 < v1:
                     load, p0 = locate(POS_LOADS, s0)
                     c, h0 = locate(CHUNKS, s0)
-                    for t in range(PACK):
-                        nc.vector.tensor_tensor(sums[step][:, t], sums_of(t, s0, n), pos_sb[load][:, t, p0 : p0 + n], ADD)
+                    g, g0 = divmod(s0, GROUP)
+                    for u in range(2):
+                        pair = slice(2 * u, 2 * u + 2)
+                        nc.vector.tensor_tensor(
+                            sums[step][:, pair], banks[2 * g + u][:, :, g0 : g0 + n], pos_sb[load][:, pair, p0 : p0 + n], ADD
+                        )
                     nc.scalar.activation(
                         h_bf[c][:, h0 : h0 + n].rearrange("p (q i) t -> p q t i", i=4),
                         sums[step][:].rearrange("p t (q i) -> p q t i", i=4),
@@ -214,7 +218,7 @@ def tile_picked_phpq_gelu_p_kernel(tc, x_words, x_scales, w1, w2, pos, offs, out
                 out=h_codes[c][:].bitcast(FP8X4), scales=h_plane[:], in_=h_bf[c][:].rearrange("p n t -> p (n t)")
             )
             nc.tensor.matmul_mx(
-                out=banks[RESULT_BANK + c][:, :n],
+                out=banks[c][:, 0, :n],
                 lhsT=w2_codes[:].bitcast(FP8X4),
                 lhsT_scale=w2_plane[:],
                 rhs=h_codes[c][:].bitcast(FP8X4),
@@ -226,14 +230,11 @@ def tile_picked_phpq_gelu_p_kernel(tc, x_words, x_scales, w1, w2, pos, offs, out
         def store(c, copy):
             s0, n = spans(CHUNKS)[c]
             res_sb = keep.tile([P, n], F32, name="res_sb%d" % c)
-            copy(res_sb[:], banks[RESULT_BANK + c][:, :n])
+            copy(res_sb[:], banks[c][:, 0, :n])
             nc.sync.dma_start(out[:, s0 : s0 + n], res_sb[:])
 
         h_codes = [keep.tile([P, n], U32, name="codes%d" % c, align_bytes=64) for c, n in enumerate(CHUNKS)]
         hidden(0, EDGE)
-        for t in range(PACK):
-            for z in range(PASSES):
-                first_product(z, t, EDGE + BANK, EDGE)
         hidden(EDGE, 2 * EDGE)
         nc.gpsimd.tensor_scalar(w2_bf[:], w2_raw[:].rearrange("p j n -> p n j"), 1.0, 0.0, MULT, ADD)
         w2_codes = keep.tile([P, N], U32, name="w2_codes", align_bytes=64)

@@ -30,6 +30,7 @@ GROUP = 256
 GROUPS = S // GROUP
 EARLY = 3
 SCALAR_M = 32
+PAIR_M = 72
 POS_LOADS = (256, 256, 256, 128, 128)
 STEPS = (64, 64) + (128,) * 7
 W2_AFTER = 2
@@ -101,9 +102,22 @@ def tile_picked_phpq_gelu_p_kernel(tc, x_words, x_scales, w1, w2, pos, offs, out
 
         w1_bf = {
             (z, a): keep.tile([P, PACK, HALF, PACK], BF16, name="w1_bf%d_%d" % (z, a), align_bytes=64)
-            for z in range(PASSES)
+            for z in range(1, PASSES)
             for a in range(2)
         }
+        pair_bf = [keep.tile([P, 2, P, PACK], BF16, name="pair_bf%d" % u, align_bytes=64) for u in range(2)]
+
+        def round_pair(copy, u, m0, m1):
+            copy(pair_bf[u][:].rearrange("p t m j -> p m j t")[:, m0:m1], raw_first[:, m0:m1, :, 2 * u : 2 * u + 2])
+
+        def quantize_pair(u):
+            cols = slice(2 * P * u, 2 * P * (u + 1))
+            nc.vector.quantize_mx(
+                out=w1_codes[0][:, cols].bitcast(FP8X4),
+                scales=w1_planes[0][:, cols],
+                in_=pair_bf[u][:].rearrange("p t m j -> p (t m j)"),
+            )
+
         w1_codes = [keep.tile([P, H], U32, name="w1_codes%d" % z, align_bytes=64) for z in range(PASSES)]
         w1_planes = [keep.tile([P, H], U8, name="w1_planes%d" % z, align_bytes=64) for z in range(PASSES)]
 
@@ -130,7 +144,7 @@ def tile_picked_phpq_gelu_p_kernel(tc, x_words, x_scales, w1, w2, pos, offs, out
 
         def first_product(z, g, opens):
             s0 = g * GROUP
-            planes = later_planes[:, s0 - GROUP : s0] if z == 1 and g > 0 else x_planes[:, s0 : s0 + GROUP]
+            planes = x_planes[z][:, s0 : s0 + GROUP]
             for t in range(PACK):
                 nc.tensor.matmul_mx(
                     out=banks[2 * g + t // 2][:, t % 2],
@@ -142,23 +156,28 @@ def tile_picked_phpq_gelu_p_kernel(tc, x_words, x_scales, w1, w2, pos, offs, out
                     stop=(not opens and t % 2 == 1),
                 )
 
-        round_w1(nc.scalar.copy, 0, raw_first, 0, 0, HALF)
-        round_w1(nc.scalar.copy, 0, raw_first, 0, HALF, HALF + SCALAR_M)
+        round_pair(nc.scalar.copy, 0, 0, P)
+        round_pair(nc.scalar.copy, 1, 0, PAIR_M)
 
-        x_planes = keep.tile([P, S], U8, name="x_planes", align_bytes=64)
-        nc.vector.tensor_copy(x_planes[:].bitcast(I32), picked_scales[:, :S].bitcast(I32))
+        x_planes = [keep.tile([P, S], U8, name="x_planes%d" % z, align_bytes=64) for z in range(PASSES)]
         for z in range(PASSES):
+            nc.vector.tensor_copy(x_planes[z][:].bitcast(I32), picked_scales[:, :S].bitcast(I32))
+
+        def move_rows(z):
             for e in range(2):
                 row = PLANE_ROW * z + e
                 nc.sync.dma_start(
-                    x_planes[row + 2 : P : QUADRANT, :].bitcast(I32),
-                    x_planes[row + LIST_ROWS : P : QUADRANT, :].bitcast(I32),
+                    x_planes[z][row + 2 : P : QUADRANT, :].bitcast(I32),
+                    x_planes[z][row + LIST_ROWS : P : QUADRANT, :].bitcast(I32),
                 )
+
+        move_rows(0)
 
         raw_late = []
         for a in range(2):
             half = shared.tile([P, half_bytes // 4], F32, name="w1_late%d" % a, align_bytes=64, offset=late_at + a * half_bytes)
             raw_late.append(load_w1(1, half[:], a * H // 2, (a + 1) * H // 2))
+        move_rows(1)
         pos_rows = pos.rearrange("(p t) s -> p t s", t=PACK)
         pos_sb = []
         for s0, n in spans(POS_LOADS):
@@ -170,9 +189,9 @@ def tile_picked_phpq_gelu_p_kernel(tc, x_words, x_scales, w1, w2, pos, offs, out
                 nc.sync.dma_start(w2_raw[:], w2.rearrange("(p j) n -> p j n", j=PACK))
 
         gather_words(0)
-        round_w1(nc.vector.tensor_copy, 0, raw_first, 0, HALF + SCALAR_M, P)
-        quantize_w1(0, 0)
-        quantize_w1(0, 1)
+        round_pair(nc.vector.tensor_copy, 1, PAIR_M, P)
+        quantize_pair(0)
+        quantize_pair(1)
         for g in range(EARLY):
             first_product(0, g, True)
         gather_words(1)
@@ -181,8 +200,6 @@ def tile_picked_phpq_gelu_p_kernel(tc, x_words, x_scales, w1, w2, pos, offs, out
         round_w1(nc.scalar.copy, 1, raw_late[1], HALF, HALF, HALF + SCALAR_M)
         round_w1(nc.vector.tensor_copy, 1, raw_late[1], HALF, HALF + SCALAR_M, P)
         quantize_w1(1, 1)
-        later_planes = shared.tile([P, S - GROUP], U8, name="later_planes", align_bytes=64, offset=late_at + half_bytes)
-        nc.vector.tensor_copy(later_planes[:].bitcast(I32), x_planes[:, GROUP:].bitcast(I32))
         for g in range(GROUPS):
             first_product(1, g, g >= EARLY)
             if g >= EARLY:

@@ -28,7 +28,7 @@ HALF = P // 2
 EDGE = 256
 GROUP = 256
 GROUPS = S // GROUP
-EARLY = 3
+EARLY_BANKS = 6
 SCALAR_M = 32
 PAIR_M = 72
 POS_LOADS = (256, 256, 256, 128, 128)
@@ -40,6 +40,10 @@ RESULT_BANK = 3
 
 def spans(widths):
     return [(sum(widths[:c]), n) for c, n in enumerate(widths)]
+
+
+def bank_tiles(b):
+    return range(2 * (b % 2), 2 * (b % 2) + 2)
 
 
 def locate(widths, s0):
@@ -101,7 +105,9 @@ def tile_picked_phpq_gelu_p_kernel(tc, x_words, x_scales, w1, w2, pos, offs, out
         nc.vector.tensor_copy(picked_scales[:, :S], scale_table[:].indirect(offsets[:]))
 
         w1_bf = {
-            (z, a): keep.tile([P, PACK, HALF, PACK], BF16, name="w1_bf%d_%d" % (z, a), align_bytes=64)
+            (z, a): shared.tile(
+                [P, PACK, HALF, PACK], BF16, name="w1_bf%d_%d" % (z, a), align_bytes=64, offset=late_at + late_bytes + a * 2 * S
+            )
             for z in range(1, PASSES)
             for a in range(2)
         }
@@ -142,10 +148,10 @@ def tile_picked_phpq_gelu_p_kernel(tc, x_words, x_scales, w1, w2, pos, offs, out
 
         banks = [psum.tile([P, 2, GROUP], F32, name="bank%d" % b) for b in range(2 * GROUPS)]
 
-        def first_product(z, g, opens):
+        def first_product(z, g, opens, tiles=range(PACK)):
             s0 = g * GROUP
-            planes = x_planes[z][:, s0 : s0 + GROUP]
-            for t in range(PACK):
+            planes = later_planes[:, s0 - GROUP : s0] if z == 1 and g > 0 else x_planes[z][:, s0 : s0 + GROUP]
+            for t in tiles:
                 nc.tensor.matmul_mx(
                     out=banks[2 * g + t // 2][:, t % 2],
                     lhsT=w1_codes[z][:, t * P : (t + 1) * P].bitcast(FP8X4),
@@ -192,18 +198,20 @@ def tile_picked_phpq_gelu_p_kernel(tc, x_words, x_scales, w1, w2, pos, offs, out
         round_pair(nc.vector.tensor_copy, 1, PAIR_M, P)
         quantize_pair(0)
         quantize_pair(1)
-        for g in range(EARLY):
-            first_product(0, g, True)
+        for b in range(EARLY_BANKS):
+            first_product(0, b // 2, True, bank_tiles(b))
         gather_words(1)
         round_w1(nc.scalar.copy, 1, raw_late[0], 0, 0, HALF)
         quantize_w1(1, 0)
         round_w1(nc.scalar.copy, 1, raw_late[1], HALF, HALF, HALF + SCALAR_M)
         round_w1(nc.vector.tensor_copy, 1, raw_late[1], HALF, HALF + SCALAR_M, P)
         quantize_w1(1, 1)
-        for g in range(GROUPS):
-            first_product(1, g, g >= EARLY)
-            if g >= EARLY:
-                first_product(0, g, False)
+        later_planes = shared.tile([P, S - GROUP], U8, name="later_planes", align_bytes=64, offset=late_at + late_bytes + 2 * S)
+        nc.vector.tensor_copy(later_planes[:].bitcast(I32), x_planes[1][:, GROUP:].bitcast(I32))
+        for b in range(2 * GROUPS):
+            first_product(1, b // 2, b >= EARLY_BANKS, bank_tiles(b))
+            if b >= EARLY_BANKS:
+                first_product(0, b // 2, False, bank_tiles(b))
 
         sums = [keep.tile([P, PACK, n], F32, name="sums%d" % c) for c, n in enumerate(STEPS)]
         h_bf = [keep.tile([P, n, PACK], BF16, name="h_bf%d" % c, align_bytes=64) for c, n in enumerate(CHUNKS)]

from contextlib import ExitStack

import concourse.mybir as mybir

K, T, S, H, N = 1024, 2048, 1024, 512, 128
FLOPS = 2 * K * H * S + 2 * H * N * S

F32 = mybir.dt.float32
BF16 = mybir.dt.bfloat16
I32 = mybir.dt.int32
U32 = mybir.dt.uint32
U16 = mybir.dt.uint16
U8 = mybir.dt.uint8
FP8X4 = mybir.dt.float8_e4m3fn_x4
GELU = mybir.ActivationFunctionType.Gelu_apprx_tanh
ADD = mybir.AluOpType.add
MULT = mybir.AluOpType.mult

P = 128
PACK = 4
PASSES = K // (P * PACK)
BANK = 512
QUADRANT = 32
LIST_ROWS = 16
PLANE_ROW = 8
HALF = P // 2

EDGE = 256
GROUP = 256
GROUPS = S // GROUP
EARLY_BANKS = 6
SCALAR_M = 32
PAIR_M = 72
POS_LOADS = (256, 256, 256, 128, 128)
STEPS = (64, 64) + (128,) * 7
W2_AFTER = 2
CHUNKS = (256, 256, 256, 128, 128)
RESULT_BANK = 3


def spans(widths):
    return [(sum(widths[:c]), n) for c, n in enumerate(widths)]


def bank_tiles(b):
    return range(2 * (b % 2), 2 * (b % 2) + 2)


def locate(widths, s0):
    c = max(c for c, (start, n) in enumerate(spans(widths)) if start <= s0)
    return c, s0 - spans(widths)[c][0]


def tile_picked_phpq_gelu_p_kernel(tc, x_words, x_scales, w1, w2, pos, offs, out):
    nc = tc.nc
    with ExitStack() as ctx:
        keep = ctx.enter_context(tc.tile_pool(name="keep", bufs=1))
        shared = ctx.enter_context(tc.tile_pool(name="shared", bufs=1))
        psum = ctx.enter_context(tc.psum_pool(name="psum", bufs=1))

        table_bytes = 4 * T
        late_at = PASSES * table_bytes
        half_bytes = 4 * PACK * H // 2
        pos_at = late_at + 2 * half_bytes
        w2_at = pos_at + 4 * PACK * S
        late_bytes = w2_at + 4 * PACK * N - late_at

        first = keep.tile([P, PACK * H], F32, name="first", align_bytes=64)
        seed = shared.tile([P, 32], F32, name="seed", align_bytes=64, offset=table_bytes - 64)
        zero_in = keep.tile([P, 1], F32, name="zero_in")
        zero_bias = keep.tile([P, 1], F32, name="zero_bias")
        nc.gpsimd.memset(first[:, 2 * H : 2 * H + 1], 0.0)
        nc.gpsimd.memset(seed[:, :1], 0.0)
        offsets = keep.tile([P, S // LIST_ROWS], U16, name="offsets")
        scale_table = keep.tile([P, T], U8, name="scale_table", align_bytes=64)
        nc.vector.memset(scale_table[:].bitcast(I32), 0)
        nc.vector.tensor_tensor(zero_in[:], first[:, 2 * H : 2 * H + 1], seed[:, :1], ADD)
        nc.scalar.activation(zero_bias[:], zero_in[:], GELU, bias=zero_in[:])

        def load_w1(z, flat, c0, c1):
            raw = flat.rearrange("p (j c) -> p j c", j=PACK)
            rows = w1[z * P * PACK : (z + 1) * P * PACK, :].rearrange("(p j) c -> p j c", j=PACK)
            nc.sync.dma_start(raw, rows[:, :, c0:c1])
            return raw.rearrange("p j (m t) -> p m j t", t=PACK)

        def load_words(z):
            table = shared.tile([P, T], I32, name="word_table%d" % z, align_bytes=64, offset=z * table_bytes)
            nc.sync.dma_start(table[:], x_words[z].rearrange("p c r -> p (c r)").bitcast(I32))
            return table

        rows_first = w1[: P * PACK, :].rearrange("(p j) c -> p (j c)", j=PACK)
        nc.sync.dma_start(first[:, :H], rows_first[:, :H])
        nc.sync.dma_start(offsets[:], offs)
        for e in range(2):
            nc.sync.dma_start(
                scale_table[e:P:PLANE_ROW, :].bitcast(I32),
                x_scales[:, e:16:2, :].rearrange("z r c -> r z c").bitcast(I32),
            )
        word_table = [load_words(0)]
        nc.sync.dma_start(first[:, H:], rows_first[:, H:])
        raw_first = first[:].rearrange("p (j m t) -> p m j t", j=PACK, t=PACK)
        word_table.append(load_words(1))

        picked_scales = shared.tile([P, late_bytes], U8, name="picked_scales", align_bytes=64, offset=late_at)
        nc.vector.tensor_copy(picked_scales[:, :S], scale_table[:].indirect(offsets[:]))

        w1_bf = {
            (z, a): shared.tile(
                [P, PACK, HALF, PACK], BF16, name="w1_bf%d_%d" % (z, a), align_bytes=64, offset=late_at + late_bytes + a * 2 * S
            )
            for z in range(1, PASSES)
            for a in range(2)
        }
        pair_bf = [keep.tile([P, 2, P, PACK], BF16, name="pair_bf%d" % u, align_bytes=64) for u in range(2)]

        def round_pair(copy, u, m0, m1):
            copy(pair_bf[u][:].rearrange("p t m j -> p m j t")[:, m0:m1], raw_first[:, m0:m1, :, 2 * u : 2 * u + 2])

        def quantize_pair(u):
            cols = slice(2 * P * u, 2 * P * (u + 1))
            nc.vector.quantize_mx(
                out=w1_codes[0][:, cols].bitcast(FP8X4),
                scales=w1_planes[0][:, cols],
                in_=pair_bf[u][:].rearrange("p t m j -> p (t m j)"),
            )

        w1_codes = [keep.tile([P, H], U32, name="w1_codes%d" % z, align_bytes=64) for z in range(PASSES)]
        w1_planes = [keep.tile([P, H], U8, name="w1_planes%d" % z, align_bytes=64) for z in range(PASSES)]

        def round_w1(copy, z, raw, raw_m, m0, m1):
            a, at = divmod(m0, HALF)
            dst = w1_bf[z, a][:].rearrange("p t m j -> p m j t")
            copy(dst[:, at : at + m1 - m0], raw[:, m0 - raw_m : m1 - raw_m])

        def quantize_w1(z, a):
            for t in range(PACK):
                cols = slice(t * P + a * HALF, t * P + (a + 1) * HALF)
                nc.vector.quantize_mx(
                    out=w1_codes[z][:, cols].bitcast(FP8X4),
                    scales=w1_planes[z][:, cols],
                    in_=w1_bf[z, a][:, t].rearrange("p m j -> p (m j)"),
                )

        picked = [keep.tile([P, S], U32, name="picked%d" % z, align_bytes=64) for z in range(PASSES)]

        def gather_words(z):
            nc.vector.tensor_copy(picked[z][:], word_table[z][:].bitcast(U32).indirect(offsets[:]))

        banks = [psum.tile([P, 2, GROUP], F32, name="bank%d" % b) for b in range(2 * GROUPS)]

        def first_product(z, g, opens, tiles=range(PACK)):
            s0 = g * GROUP
            planes = later_planes[:, s0 - GROUP : s0] if z == 1 and g > 0 else x_planes[z][:, s0 : s0 + GROUP]
            for t in tiles:
                nc.tensor.matmul_mx(
                    out=banks[2 * g + t // 2][:, t % 2],
                    lhsT=w1_codes[z][:, t * P : (t + 1) * P].bitcast(FP8X4),
                    lhsT_scale=w1_planes[z][:, t * P : (t + 1) * P],
                    rhs=picked[z][:, s0 : s0 + GROUP].bitcast(FP8X4),
                    rhs_scale=planes[PLANE_ROW * z :],
                    start=(opens and t % 2 == 0),
                    stop=(not opens and t % 2 == 1),
                )

        round_pair(nc.scalar.copy, 0, 0, P)
        round_pair(nc.scalar.copy, 1, 0, PAIR_M)

        x_planes = [keep.tile([P, S], U8, name="x_planes%d" % z, align_bytes=64) for z in range(PASSES)]
        for z in range(PASSES):
            nc.vector.tensor_copy(x_planes[z][:].bitcast(I32), picked_scales[:, :S].bitcast(I32))

        def move_rows(z):
            for e in range(2):
                row = PLANE_ROW * z + e
                nc.sync.dma_start(
                    x_planes[z][row + 2 : P : QUADRANT, :].bitcast(I32),
                    x_planes[z][row + LIST_ROWS : P : QUADRANT, :].bitcast(I32),
                )

        move_rows(0)

        raw_late = []
        for a in range(2):
            half = shared.tile([P, half_bytes // 4], F32, name="w1_late%d" % a, align_bytes=64, offset=late_at + a * half_bytes)
            raw_late.append(load_w1(1, half[:], a * H // 2, (a + 1) * H // 2))
        move_rows(1)
        pos_rows = pos.rearrange("(p t) s -> p t s", t=PACK)
        pos_sb = []
        for s0, n in spans(POS_LOADS):
            piece = shared.tile([P, PACK, n], F32, name="pos%d" % len(pos_sb), align_bytes=64, offset=pos_at + 4 * PACK * s0)
            nc.sync.dma_start(piece[:], pos_rows[:, :, s0 : s0 + n])
            pos_sb.append(piece)
            if len(pos_sb) == W2_AFTER:
                w2_raw = shared.tile([P, PACK, N], F32, name="w2_raw", align_bytes=64, offset=w2_at)
                nc.sync.dma_start(w2_raw[:], w2.rearrange("(p j) n -> p j n", j=PACK))

        gather_words(0)
        round_pair(nc.vector.tensor_copy, 1, PAIR_M, P)
        quantize_pair(0)
        quantize_pair(1)
        for b in range(EARLY_BANKS):
            first_product(0, b // 2, True, bank_tiles(b))
        gather_words(1)
        round_w1(nc.scalar.copy, 1, raw_late[0], 0, 0, HALF)
        quantize_w1(1, 0)
        round_w1(nc.scalar.copy, 1, raw_late[1], HALF, HALF, HALF + SCALAR_M)
        round_w1(nc.vector.tensor_copy, 1, raw_late[1], HALF, HALF + SCALAR_M, P)
        quantize_w1(1, 1)
        later_planes = shared.tile([P, S - GROUP], U8, name="later_planes", align_bytes=64, offset=late_at + late_bytes + 2 * S)
        nc.vector.tensor_copy(later_planes[:].bitcast(I32), x_planes[1][:, GROUP:].bitcast(I32))
        for b in range(2 * GROUPS):
            first_product(1, b // 2, b >= EARLY_BANKS, bank_tiles(b))
            if b >= EARLY_BANKS:
                first_product(0, b // 2, False, bank_tiles(b))

        sums = [keep.tile([P, PACK, n], F32, name="sums%d" % c) for c, n in enumerate(STEPS)]
        h_bf = [keep.tile([P, n, PACK], BF16, name="h_bf%d" % c, align_bytes=64) for c, n in enumerate(CHUNKS)]
        w2_bf = keep.tile([P, N, PACK], BF16, name="w2_bf", align_bytes=64)
        w2_plane = keep.tile([P, N], U8, name="w2_plane", align_bytes=64)

        def hidden(v0, v1):
            for step, (s0, n) in enumerate(spans(STEPS)):
                if v0 <= s0 < v1:
                    load, p0 = locate(POS_LOADS, s0)
                    c, h0 = locate(CHUNKS, s0)
                    g, g0 = divmod(s0, GROUP)
                    for u in range(2):
                        pair = slice(2 * u, 2 * u + 2)
                        nc.vector.tensor_tensor(
                            sums[step][:, pair], banks[2 * g + u][:, :, g0 : g0 + n], pos_sb[load][:, pair, p0 : p0 + n], ADD
                        )
                    nc.scalar.activation(
                        h_bf[c][:, h0 : h0 + n].rearrange("p (q i) t -> p q t i", i=4),
                        sums[step][:].rearrange("p t (q i) -> p q t i", i=4),
                        GELU,
                        bias=zero_bias[:],
                    )

        def second_product(c):
            n = CHUNKS[c]
            h_plane = keep.tile([P, n], U8, name="h_plane%d" % c, align_bytes=64)
            nc.vector.quantize_mx(
                out=h_codes[c][:].bitcast(FP8X4), scales=h_plane[:], in_=h_bf[c][:].rearrange("p n t -> p (n t)")
            )
            nc.tensor.matmul_mx(
                out=banks[c][:, 0, :n],
                lhsT=w2_codes[:].bitcast(FP8X4),
                lhsT_scale=w2_plane[:],
                rhs=h_codes[c][:].bitcast(FP8X4),
                rhs_scale=h_plane[:],
                start=True,
                stop=True,
            )

        def store(c, copy):
            s0, n = spans(CHUNKS)[c]
            res_sb = keep.tile([P, n], F32, name="res_sb%d" % c)
            copy(res_sb[:], banks[c][:, 0, :n])
            nc.sync.dma_start(out[:, s0 : s0 + n], res_sb[:])

        h_codes = [keep.tile([P, n], U32, name="codes%d" % c, align_bytes=64) for c, n in enumerate(CHUNKS)]
        hidden(0, EDGE)
        hidden(EDGE, 2 * EDGE)
        nc.gpsimd.tensor_scalar(w2_bf[:], w2_raw[:].rearrange("p j n -> p n j"), 1.0, 0.0, MULT, ADD)
        w2_codes = keep.tile([P, N], U32, name="w2_codes", align_bytes=64)
        nc.vector.quantize_mx(out=w2_codes[:].bitcast(FP8X4), scales=w2_plane[:], in_=w2_bf[:].rearrange("p n j -> p (n j)"))
        second_product(0)
        store(0, nc.scalar.copy)
        hidden(2 * EDGE, 3 * EDGE)
        second_product(1)
        hidden(3 * EDGE, S)
        second_product(2)
        second_product(3)
        store(1, nc.vector.tensor_copy)
        second_product(4)
        store(2, nc.scalar.copy)
        store(3, nc.scalar.copy)
        store(4, nc.vector.tensor_copy)
